import numpy as np
import ml_dtypes


def mxq(x, axis, fmt="e4m3"):
    dtype, down = {"e4m3": (ml_dtypes.float8_e4m3fn, 7), "e5m2": (ml_dtypes.float8_e5m2, 14)}[fmt]
    v = np.moveaxis(np.asarray(x, np.float32).astype(ml_dtypes.bfloat16).astype(np.float64), axis, -1)
    blocks = v.reshape(v.shape[:-1] + (-1, 32))
    amax = np.abs(blocks).max(-1, keepdims=True)
    byte = np.maximum(np.where(amax > 0, np.frexp(amax)[1] - 1 + 127, 0) - down, 1)
    scale = np.exp2(byte - 127.0)
    codes = (blocks / scale).astype(np.float32).astype(dtype).astype(np.float64)
    return np.moveaxis((codes * scale).reshape(v.shape), -1, axis)


WIDE = False


def mx_kscale(k):
    if not WIDE:
        return np.ones(k)
    levels = np.array([10, -10, 5, -5, 0])
    if k % 512:
        return np.exp2(np.random.permutation(np.resize(levels, k // 32))).repeat(32)
    a = np.empty((k // 512, 16))
    for p in range(k // 512):
        a[p, :8] = np.random.permutation(np.resize(levels, 8))
        for g in range(8):
            far = levels[np.abs(levels - a[p, g]) >= 10]
            a[p, g + 8] = far[np.random.randint(len(far))]
    return np.exp2(a.ravel()).repeat(32)


BF16 = ml_dtypes.bfloat16


def bf(x):
    return np.asarray(x, np.float32).astype(BF16)


def f64(x):
    return np.asarray(x).astype(np.float64)


E2M1 = np.array([0.0, 0.5, 1.0, 1.5, 2.0, 3.0, 4.0, 6.0, -0.0, -0.5, -1.0, -1.5, -2.0, -3.0, -4.0, -6.0])


def pack_weight(w, fmt):
    k, n = w.shape
    w = f64(bf(w)).reshape(k // 32, 32, n)
    amax = np.abs(w).max(1)
    if fmt == "e4m3":
        byte = np.frexp(amax)[1] - 1 + 127 - 7
    else:
        mant, ex = np.frexp(amax / 6.0)
        byte = np.where(mant > 0.5, ex, ex - 1) + 127
    byte = np.clip(np.where(amax > 0, byte, 1), 1, 254)
    scaled = (w * np.exp2(127.0 - byte)[:, None, :]).reshape(k, n).astype(np.float32)
    by_word = np.ascontiguousarray(scaled.reshape(k // 512, 128, 4, n).transpose(0, 1, 3, 2))
    if fmt == "e4m3":
        words = by_word.astype(ml_dtypes.float8_e4m3fn).view(np.uint8)
    else:
        c = by_word.astype(ml_dtypes.float4_e2m1fn).view(np.uint8) & 0xF
        words = c[..., 0::2] | (c[..., 1::2] << 4)
    return np.ascontiguousarray(words), np.ascontiguousarray(byte.astype(np.uint8).reshape(k // 512, 16, n))


def unpack_weight(words, scales, fmt):
    g, p, n, _ = words.shape
    if fmt == "e4m3":
        vals = np.ascontiguousarray(words).view(ml_dtypes.float8_e4m3fn).astype(np.float64)
    else:
        nib = np.empty((g, p, n, 4), np.uint8)
        nib[..., 0::2] = words & 0xF
        nib[..., 1::2] = words >> 4
        vals = E2M1[nib]
    vals = vals * np.repeat(np.exp2(scales.astype(np.float64) - 127.0), 8, axis=1)[..., None]
    return vals.transpose(0, 1, 3, 2).reshape(g * 512, n)
def pack4(w):
    words, scales = pack_weight(w, "e2m1")
    return words.reshape(words.shape[0], 128, -1), scales


def unpack4(words, scales):
    return unpack_weight(words.reshape(words.shape[0], 128, -1, 2), scales, "e2m1")


M, K, N, P = 2048, 1536, 1024, 512


def draw0():
    s = mx_kscale(K)
    t = mx_kscale(M)
    patches = np.random.standard_normal((M, K)) * s
    comps = np.random.standard_normal((K, N)) / np.sqrt(K) / s[:, None]
    centre = 0.3 * np.random.standard_normal(N)
    weight = (1 + 0.1 * np.random.standard_normal(M)) * t
    filt = np.random.standard_normal((M, P)) / np.sqrt(M) / t[:, None]
    filt_words, filt_scales = pack4(filt)
    return {"patches": bf(patches),
            "comps": bf(comps),
            "centre": bf(centre),
            "weight": bf(weight),
            "filt_words": filt_words,
            "filt_scales": filt_scales}


def core(patches, comps, centre, weight, filt_words, filt_scales):
    filt = unpack4(filt_words, filt_scales)
    e = (mxq(f64(patches), 1, "e4m3") @ mxq(f64(comps), 0, "e4m3")) - f64(centre)
    v = e ** 2 * f64(weight)[:, None]
    return filt.T @ mxq(v, 0, "e4m3")


def e4m3fn_bytes(y):
    return np.clip(np.asarray(y, np.float64), -448.0, 448.0).astype(np.float32).astype(ml_dtypes.float8_e4m3fn).view(np.uint8)


def e4m3fn_values(b):
    return np.asarray(b, np.uint8).view(ml_dtypes.float8_e4m3fn).astype(np.float64)


def setup_inputs():
    d = draw0()
    x0 = np.asarray(d['patches']).astype(np.float64)
    s = (np.max(np.abs(x0), axis=(0,), keepdims=True) / 448.0).astype(np.float32)
    out = {}
    for k, v in d.items():
        if k == 'patches':
            out['patches_bytes'] = e4m3fn_bytes(x0 / s.astype(np.float64))
            out['patches_scale'] = s
        else:
            out[k] = v
    return out


def reference(patches_bytes, patches_scale, comps, centre, weight, filt_words, filt_scales):
    return core(e4m3fn_values(patches_bytes) * patches_scale.astype(np.float64), comps, centre, weight, filt_words, filt_scales)

@@ -1,0 +1,388 @@
+from contextlib import ExitStack
+
+import concourse.mybir as mybir
+from concourse.masks import make_identity
+
+M, K, N, PF = 2048, 1536, 1024, 512
+FLOPS = 2 * M * K * N + 2 * M * N * PF
+
+F32 = mybir.dt.float32
+BF16 = mybir.dt.bfloat16
+I32 = mybir.dt.int32
+U32 = mybir.dt.uint32
+U8 = mybir.dt.uint8
+F8 = mybir.dt.float8_e4m3fn
+FP8X4 = mybir.dt.float8_e4m3fn_x4
+FP4X4 = mybir.dt.float4_e2m1fn_x4
+ACT = mybir.ActivationFunctionType
+ALU = mybir.AluOpType
+
+P = 128
+C = K // 512
+G = M // 512
+NT = N // P
+PT = PF // P
+UNITS = M // 256
+XT_OF = ((0,), (1, 2))
+CH = 4
+
+
+def tile_pca_residual_map_s13_kernel(
+    tc, patches_bytes, patches_scale, comps, centre, weight, filt_words, filt_scales, out
+):
+    nc = tc.nc
+    with ExitStack() as ctx:
+        keep = ctx.enter_context(tc.tile_pool(name="keep", bufs=1))
+        xb_pool = ctx.enter_context(tc.tile_pool(name="xb_pool", bufs=5))
+        xg_pool = ctx.enter_context(tc.tile_pool(name="xg_pool", bufs=6))
+        cg_pool = ctx.enter_context(tc.tile_pool(name="cg_pool", bufs=3))
+        q_pool = ctx.enter_context(tc.tile_pool(name="q_pool", bufs=4))
+        vt_pool = ctx.enter_context(tc.tile_pool(name="vt_pool", bufs=8))
+        vg_pool = ctx.enter_context(tc.tile_pool(name="vg_pool", bufs=3))
+        res_pool = ctx.enter_context(tc.tile_pool(name="res_pool", bufs=8))
+        psum = ctx.enter_context(tc.psum_pool(name="psum", bufs=1))
+        ctx.enter_context(tc.manual_schedule())
+
+        def bank(tag, dtype=F32):
+            return psum.tile([P, 512 if dtype == F32 else 1024], dtype, name=tag)
+
+        scale_bc = keep.tile([P, K], F32, name="scale_bc")
+        for c in range(C):
+            cols = slice(512 * c, 512 * (c + 1))
+            nc.scalar.dma_start(
+                out=scale_bc[:, cols],
+                in_=patches_scale[:, cols].rearrange("o k -> (o k)").partition_broadcast(P),
+            )
+
+        x_rows = patches_bytes.rearrange("(i a p) k -> i p a k", a=2, p=P)
+        x_bytes = []
+        for i in range(UNITS):
+            xby = keep.tile([P, 2, K], U8, name="xby%d" % i)
+            x_bytes.append(xby)
+        c_rows = comps.rearrange("(c p t) n -> c p t n", p=P, t=4)
+        c_raw = {}
+        for c in range(C):
+            for h in range(2):
+                craw = keep.tile([P, 4, 512], BF16, name="craw%d%d" % (c, h))
+                c_raw[c, h] = craw
+        weight_bc = keep.tile([P, M], BF16, name="weight_bc")
+        weight_upe = keep.tile([P, G, 2, 256], BF16, name="weight_upe")
+        centre_rows = keep.tile([P, P], BF16, name="centre_rows")
+        f_words = keep.tile([P, G, 2 * PF], U8, align_bytes=64, name="f_words")
+        f_scales = keep.tile([P, G, PF], U8, align_bytes=64, name="f_scales")
+
+        ident_bf = keep.tile([P, P], BF16, name="ident_bf")
+        ident_f32 = keep.tile([P, P], F32, name="ident_f32")
+        nc.gpsimd.memset(centre_rows[:], 0.0)
+        make_identity(nc, ident_bf[:])
+        make_identity(nc, ident_f32[:])
+        nc.gpsimd.memset(f_scales[:].rearrange("p g n -> p (g n)").bitcast(I32), 0)
+
+        def load_x(i):
+            nc.sync.dma_start(out=x_bytes[i][:], in_=x_rows[i])
+
+        def load_c(c, h):
+            nc.sync.dma_start(out=c_raw[c, h][:], in_=c_rows[c][:, :, 512 * h : 512 * (h + 1)])
+
+        def load_w(g):
+            cols = slice(512 * g, 512 * (g + 1))
+            nc.sync.dma_start(out=weight_bc[:, cols], in_=weight[cols].partition_broadcast(P))
+
+        load_x(0)
+        nc.scalar.dma_start(out=centre_rows[0:NT, :], in_=centre.rearrange("(j p) -> j p", p=P))
+        for c in range(C):
+            load_c(c, 0)
+        load_w(0)
+        load_x(1)
+        for c in range(C):
+            load_c(c, 1)
+        for g in range(1, G):
+            load_w(g)
+        load_x(2)
+        load_x(3)
+        nc.sync.dma_start(
+            out=f_words[:].bitcast(I32), in_=filt_words.bitcast(I32).rearrange("g p x -> p g x")
+        )
+        f_scale_rows = filt_scales.bitcast(I32).rearrange("g q n -> q g n")
+        for quad in range(4):
+            nc.sync.dma_start(
+                out=f_scales[32 * quad : 32 * quad + 4, :, :].bitcast(I32),
+                in_=f_scale_rows[4 * quad : 4 * quad + 4],
+            )
+        for i in range(4, UNITS):
+            load_x(i)
+
+        c_codes = keep.tile([P, C, N], U32, align_bytes=64, name="c_codes")
+        c_scales = keep.tile([P, C, N], U8, align_bytes=64, name="c_scales")
+        xc_pool = ctx.enter_context(tc.tile_pool(name="xc_pool", bufs=2))
+        v_codes = keep.tile([P, G, N], U32, align_bytes=64, name="v_codes")
+        v_scales = keep.tile([P, G, N], U8, align_bytes=64, name="v_scales")
+        neg_centre = keep.tile([P, NT], F32, name="neg_centre")
+
+        xb_of = {}
+        xbank_of = {}
+        xg_of = {}
+        x_codes = {}
+        x_scales = {}
+        cg_of = {}
+        cbank_of = {}
+        m_of = {}
+        q_of = {}
+        vt_of = {}
+        vbank_of = {}
+        vg_of = {}
+        o_of = {}
+        counter = {"t": 0, "d": 0, "m": 0}
+
+        def next_t():
+            counter["t"] += 1
+            return bank("t%d" % (counter["t"] % 2))
+
+        def widen(r, pieces=1):
+            xb = xb_pool.tile([P, K], BF16, name="xb")
+            xb_of[r] = xb
+            w = K // pieces
+            for s in range(pieces):
+                nc.vector.tensor_tensor(
+                    out=xb[:, w * s : w * (s + 1)],
+                    in0=x_bytes[r // 2][:, r % 2, w * s : w * (s + 1)].bitcast(F8),
+                    in1=scale_bc[:, w * s : w * (s + 1)],
+                    op=ALU.mult,
+                )
+
+        def x_transpose(i, c):
+            b = next_t()
+            xbank_of[i, c] = b
+            for a in range(2):
+                words = xb_of[2 * i + a][:].bitcast(F32)
+                for u in range(2):
+                    lo = 256 * a + 128 * u
+                    nc.tensor.transpose(b[:, lo : lo + P], words[:, 256 * c + u : 256 * (c + 1) : 2], ident_f32[:])
+
+        def x_exit(i, c):
+            xg = xg_pool.tile([P, 1024], BF16, align_bytes=64, name="xg")
+            xg_of[i, c] = xg
+            nc.scalar.copy(
+                out=xg[:].bitcast(F32).rearrange("p (a r u) -> p a r u", a=2, u=2),
+                in_=xbank_of[i, c][:].rearrange("p (a u r) -> p a r u", a=2, u=2),
+            )
+
+        def x_quant(i, c):
+            if c == 0:
+                xc = xc_pool.tile([P, C, 256], U32, align_bytes=64, name="xc")
+                xs = xc_pool.tile([P, C, 256], U8, align_bytes=64, name="xs")
+                x_codes[i] = xc
+                x_scales[i] = xs
+            nc.vector.quantize_mx(
+                out=x_codes[i][:, c, :].bitcast(FP8X4), scales=x_scales[i][:, c, :], in_=xg_of[i, c][:]
+            )
+
+        def c_interleave(c, h):
+            for b in range(2):
+                counter["d"] += 1
+                bk = bank("o%d" % (counter["d"] % 4), BF16)
+                cbank_of[c, h, b] = bk
+                for s in range(2):
+                    n0 = 256 * b + 128 * s
+                    nc.tensor.matmul(
+                        bk[:, 512 * s : 512 * (s + 1)],
+                        lhsT=ident_bf[:],
+                        rhs=c_raw[c, h][:, :, n0 : n0 + P].rearrange("p t n -> p n t"),
+                        start=True,
+                        stop=True,
+                    )
+
+        def c_exit(c, h):
+            cg = cg_pool.tile([P, 2048], BF16, align_bytes=64, name="cg")
+            cg_of[c, h] = cg
+            for b in range(2):
+                nc.scalar.copy(out=cg[:, 1024 * b : 1024 * (b + 1)], in_=cbank_of[c, h, b][:])
+
+        def c_quant(c, h):
+            cols = slice(512 * h, 512 * (h + 1))
+            nc.vector.quantize_mx(
+                out=c_codes[:, c, cols].bitcast(FP8X4), scales=c_scales[:, c, cols], in_=cg_of[c, h][:]
+            )
+
+        def mm(i, j):
+            counter["m"] += 1
+            b = bank("m%d" % (counter["m"] % 2))
+            m_of[i, j] = b
+            for s in range(2):
+                cols = slice(P * (2 * j + s), P * (2 * j + s + 1))
+                for c in range(C):
+                    nc.tensor.matmul_mx(
+                        out=b[:, 256 * s : 256 * (s + 1)],
+                        lhsT=c_codes[:, c, cols].bitcast(FP8X4),
+                        lhsT_scale=c_scales[:, c, cols],
+                        rhs=x_codes[i][:, c, :].bitcast(FP8X4),
+                        rhs_scale=x_scales[i][:, c, :],
+                        start=(c == 0),
+                        stop=(c == C - 1),
+                    )
+
+        def square(i, j):
+            qt = q_pool.tile([P, 512], F32, name="qt")
+            q_of[i, j] = qt
+            for s in range(2):
+                nt = 2 * j + s
+                half = slice(256 * s, 256 * (s + 1))
+                nc.scalar.activation(
+                    out=qt[:, half].rearrange("n (u p e) -> n u p e", u=2, e=2),
+                    in_=m_of[i, j][:, half].rearrange("n (p u e) -> n u p e", u=2, e=2),
+                    func=ACT.Square,
+                    bias=neg_centre[:, nt : nt + 1],
+                    scale=1.0,
+                )
+
+        def weight_order(g):
+            nc.scalar.copy(
+                out=weight_upe[:, g].rearrange("n u (p e) -> n u p e", e=2),
+                in_=weight_bc[:, 512 * g : 512 * (g + 1)].rearrange("n (p u e) -> n u p e", u=2, e=2),
+            )
+
+        def times_weight(i, j):
+            g = i // 2
+            lo = 128 * (i % 2)
+            if i % 2 == 0:
+                vt = vt_pool.tile([P, 2, 2, 256], BF16, name="vt")
+                vt_of[g, j] = vt
+            w = weight_upe[:, g, :, lo : lo + 128]
+            nc.vector.tensor_tensor(
+                out=vt_of[g, j][:, :, :, lo : lo + 128],
+                in0=q_of[i, j][:].rearrange("n (s u x) -> n s u x", s=2, u=2),
+                in1=w.unsqueeze(1).to_broadcast([P, 2, 2, 128]),
+                op=ALU.mult,
+            )
+
+        def v_transpose(g, j):
+            b = next_t()
+            vbank_of[g, j] = b
+            words = vt_of[g, j][:].rearrange("n s u x -> n (s u x)").bitcast(F32)
+            for s in range(4):
+                nc.tensor.transpose(b[:, P * s : P * (s + 1)], words[:, P * s : P * (s + 1)], ident_f32[:])
+
+        def v_exit(g, j):
+            vg = vg_pool.tile([P, 1024], BF16, align_bytes=64, name="vg")
+            vg_of[g, j] = vg
+            nc.scalar.copy(
+                out=vg[:].bitcast(F32).rearrange("p (a r u) -> p a r u", a=2, u=2),
+                in_=vbank_of[g, j][:].rearrange("p (a u r) -> p a r u", a=2, u=2),
+            )
+
+        def v_quant(g, j):
+            cols = slice(256 * j, 256 * (j + 1))
+            nc.vector.quantize_mx(
+                out=v_codes[:, g, cols].bitcast(FP8X4), scales=v_scales[:, g, cols], in_=vg_of[g, j][:]
+            )
+
+        def contrast(g, h, tags, pts=range(PT)):
+            for pt in pts:
+                if g == 0:
+                    o_of[h, pt] = bank(tags[pt])
+                nc.tensor.matmul_mx(
+                    out=o_of[h, pt][:],
+                    lhsT=f_words[:, g, 2 * P * pt : 2 * P * (pt + 1)].bitcast(FP4X4),
+                    lhsT_scale=f_scales[:, g, P * pt : P * (pt + 1)],
+                    rhs=v_codes[:, g, 512 * h : 512 * (h + 1)].bitcast(FP8X4),
+                    rhs_scale=v_scales[:, g, 512 * h : 512 * (h + 1)],
+                    start=(g == 0),
+                    stop=(g == G - 1),
+                )
+
+        def store(h, pt):
+            res = res_pool.tile([P, 512], F32, name="res")
+            if pt % 2 == 0:
+                nc.scalar.copy(out=res[:], in_=o_of[h, pt][:])
+            else:
+                nc.vector.tensor_copy(out=res[:], in_=o_of[h, pt][:])
+            nc.sync.dma_start(out=out[P * pt : P * (pt + 1), 512 * h : 512 * (h + 1)], in_=res[:])
+
+        widen(0, 3)
+        widen(1, 3)
+        c_interleave(0, 0)
+        c_exit(0, 0)
+        c_interleave(1, 0)
+        x_transpose(0, 0)
+        x_exit(0, 0)
+        c_exit(1, 0)
+        x_transpose(0, 1)
+        x_exit(0, 1)
+        x_transpose(0, 2)
+        x_exit(0, 2)
+        c_interleave(2, 0)
+        c_exit(2, 0)
+        widen(2)
+        c_quant(0, 0)
+        x_quant(0, 0)
+        c_quant(1, 0)
+        x_quant(0, 1)
+        x_quant(0, 2)
+        c_quant(2, 0)
+        centre_bank = bank("m0", BF16)
+        nc.tensor.transpose(centre_bank[:, 0:P], centre_rows[:], ident_bf[:])
+        nc.scalar.activation(out=neg_centre[:], in_=centre_bank[:, 0:NT], func=ACT.Copy, scale=-1.0)
+        weight_order(0)
+
+        for i in range(UNITS):
+            last = i == UNITS - 1
+            even = i % 2 == 0 and i > 0
+            g = i // 2 - 1
+            for j in range(CH):
+                mm(i, j)
+                square(i, j)
+                if i == 0 and j == 0:
+                    for c in range(C):
+                        c_interleave(c, 1)
+                        c_exit(c, 1)
+                if j == 1:
+                    times_weight(i, 0)
+                if j < 2 and 2 * i + 3 + j < 2 * UNITS:
+                    widen(2 * i + 3 + j)
+                if i == 0 and j == 0:
+                    for c in range(C):
+                        c_quant(c, 1)
+                if j < 2 and even:
+                    for jj in (2 * j, 2 * j + 1):
+                        v_transpose(g, jj)
+                        v_exit(g, jj)
+                if j < 2 and not last:
+                    for c in XT_OF[j]:
+                        x_transpose(i + 1, c)
+                        x_exit(i + 1, c)
+                if j < 2 and even:
+                    for jj in (2 * j, 2 * j + 1):
+                        v_quant(g, jj)
+                if j >= 2:
+                    times_weight(i, j - 1)
+                if j == 2 and not last:
+                    for c in range(C):
+                        x_quant(i + 1, c)
+                if j >= 2 and last:
+                    v_transpose(G - 1, j - 2)
+                    v_exit(G - 1, j - 2)
+            if even:
+                contrast(g, 0, ["o0", "o1", "o2", "o3"])
+            times_weight(i, 3)
+            if i % 2 == 1 and not last:
+                weight_order(i // 2 + 1)
+
+        g = G - 1
+        v_quant(g, 0)
+        v_transpose(g, 2)
+        v_exit(g, 2)
+        v_quant(g, 1)
+        contrast(g, 0, None)
+        for gg in range(G - 1):
+            contrast(gg, 1, ["m0", "m1"], range(2))
+        v_transpose(g, 3)
+        v_exit(g, 3)
+        v_quant(g, 2)
+        for pt in range(PT):
+            store(0, pt)
+        for gg in range(G - 1):
+            contrast(gg, 1, [None, None, "o0", "o1"], range(2, PT))
+        v_quant(g, 3)
+        contrast(g, 1, None)
+        for pt in range(PT):
+            store(1, pt)

@@ -23,7 +23,6 @@ G = M // 512
 NT = N // P
 PT = PF // P
 UNITS = M // 256
-XT_OF = ((0,), (1, 2))
 CH = 4
 
 
@@ -33,15 +32,14 @@ def tile_pca_residual_map_s13_kernel(
     nc = tc.nc
     with ExitStack() as ctx:
         keep = ctx.enter_context(tc.tile_pool(name="keep", bufs=1))
-        xb_pool = ctx.enter_context(tc.tile_pool(name="xb_pool", bufs=5))
+        xb_pool = ctx.enter_context(tc.tile_pool(name="xb_pool", bufs=8))
         xg_pool = ctx.enter_context(tc.tile_pool(name="xg_pool", bufs=6))
         cg_pool = ctx.enter_context(tc.tile_pool(name="cg_pool", bufs=3))
-        q_pool = ctx.enter_context(tc.tile_pool(name="q_pool", bufs=4))
+        q_pool = ctx.enter_context(tc.tile_pool(name="q_pool", bufs=10))
         vt_pool = ctx.enter_context(tc.tile_pool(name="vt_pool", bufs=8))
-        vg_pool = ctx.enter_context(tc.tile_pool(name="vg_pool", bufs=3))
+        vg_pool = ctx.enter_context(tc.tile_pool(name="vg_pool", bufs=5))
         res_pool = ctx.enter_context(tc.tile_pool(name="res_pool", bufs=8))
         psum = ctx.enter_context(tc.psum_pool(name="psum", bufs=1))
-        ctx.enter_context(tc.manual_schedule())
 
         def bank(tag, dtype=F32):
             return psum.tile([P, 512 if dtype == F32 else 1024], dtype, name=tag)
@@ -132,6 +130,7 @@ def tile_pca_residual_map_s13_kernel(
         vbank_of = {}
         vg_of = {}
         o_of = {}
+        part_of = {}
         counter = {"t": 0, "d": 0, "m": 0}
 
         def next_t():
@@ -276,9 +275,9 @@ def tile_pca_residual_map_s13_kernel(
                 out=v_codes[:, g, cols].bitcast(FP8X4), scales=v_scales[:, g, cols], in_=vg_of[g, j][:]
             )
 
-        def contrast(g, h, tags, pts=range(PT)):
+        def contrast(g, h, tags, pts=range(PT), first=0):
             for pt in pts:
-                if g == 0:
+                if g == first:
                     o_of[h, pt] = bank(tags[pt])
                 nc.tensor.matmul_mx(
                     out=o_of[h, pt][:],
@@ -286,13 +285,31 @@ def tile_pca_residual_map_s13_kernel(
                     lhsT_scale=f_scales[:, g, P * pt : P * (pt + 1)],
                     rhs=v_codes[:, g, 512 * h : 512 * (h + 1)].bitcast(FP8X4),
                     rhs_scale=v_scales[:, g, 512 * h : 512 * (h + 1)],
-                    start=(g == 0),
+                    start=(g == first),
                     stop=(g == G - 1),
                 )
 
+        def park(pt):
+            b = next_t()
+            for g in range(2):
+                nc.tensor.matmul_mx(
+                    out=b[:],
+                    lhsT=f_words[:, g, 2 * P * pt : 2 * P * (pt + 1)].bitcast(FP4X4),
+                    lhsT_scale=f_scales[:, g, P * pt : P * (pt + 1)],
+                    rhs=v_codes[:, g, 512:1024].bitcast(FP8X4),
+                    rhs_scale=v_scales[:, g, 512:1024],
+                    start=(g == 0),
+                    stop=(g == 1),
+                )
+            part = keep.tile([P, 512], F32, name="part%d" % pt)
+            part_of[pt] = part
+            nc.scalar.copy(out=part[:], in_=b[:])
+
         def store(h, pt):
             res = res_pool.tile([P, 512], F32, name="res")
-            if pt % 2 == 0:
+            if h == 1:
+                nc.vector.tensor_tensor(out=res[:], in0=o_of[h, pt][:], in1=part_of[pt][:], op=ALU.add)
+            elif pt % 2 == 0:
                 nc.scalar.copy(out=res[:], in_=o_of[h, pt][:])
             else:
                 nc.vector.tensor_copy(out=res[:], in_=o_of[h, pt][:])
@@ -323,66 +340,67 @@ def tile_pca_residual_map_s13_kernel(
         nc.tensor.transpose(centre_bank[:, 0:P], centre_rows[:], ident_bf[:])
         nc.scalar.activation(out=neg_centre[:], in_=centre_bank[:, 0:NT], func=ACT.Copy, scale=-1.0)
         weight_order(0)
+        widen(3)
 
-        for i in range(UNITS):
-            last = i == UNITS - 1
-            even = i % 2 == 0 and i > 0
-            g = i // 2 - 1
-            for j in range(CH):
+        GROUPS = 2 * UNITS
+        for t in range(GROUPS):
+            i, b = t // 2, t % 2
+            for j in (2 * b, 2 * b + 1):
                 mm(i, j)
                 square(i, j)
-                if i == 0 and j == 0:
-                    for c in range(C):
-                        c_interleave(c, 1)
-                        c_exit(c, 1)
-                if j == 1:
-                    times_weight(i, 0)
-                if j < 2 and 2 * i + 3 + j < 2 * UNITS:
-                    widen(2 * i + 3 + j)
-                if i == 0 and j == 0:
-                    for c in range(C):
-                        c_quant(c, 1)
-                if j < 2 and even:
-                    for jj in (2 * j, 2 * j + 1):
-                        v_transpose(g, jj)
-                        v_exit(g, jj)
-                if j < 2 and not last:
-                    for c in XT_OF[j]:
-                        x_transpose(i + 1, c)
-                        x_exit(i + 1, c)
-                if j < 2 and even:
-                    for jj in (2 * j, 2 * j + 1):
-                        v_quant(g, jj)
-                if j >= 2:
-                    times_weight(i, j - 1)
-                if j == 2 and not last:
-                    for c in range(C):
-                        x_quant(i + 1, c)
-                if j >= 2 and last:
-                    v_transpose(G - 1, j - 2)
-                    v_exit(G - 1, j - 2)
-            if even:
-                contrast(g, 0, ["o0", "o1", "o2", "o3"])
-            times_weight(i, 3)
-            if i % 2 == 1 and not last:
-                weight_order(i // 2 + 1)
+            if t == 0:
+                for c in range(C):
+                    c_interleave(c, 1)
+                    c_exit(c, 1)
+                    c_quant(c, 1)
+            if t > 0:
+                times_weight((t - 1) // 2, 2 * ((t - 1) % 2))
+            if t + 4 < 2 * UNITS:
+                widen(t + 4)
+            if b == 0 and i + 1 < UNITS:
+                for c in range(C):
+                    x_transpose(i + 1, c)
+                    x_exit(i + 1, c)
+            if t > 0:
+                times_weight((t - 1) // 2, 2 * ((t - 1) % 2) + 1)
+            if b == 1 and i + 1 < UNITS:
+                for c in range(C):
+                    x_quant(i + 1, c)
+            if t % 4 == 1 and t > 4:
+                for jj in range(CH):
+                    v_transpose(t // 4 - 1, jj)
+                    v_exit(t // 4 - 1, jj)
+            if t % 4 == 2 and t > 4:
+                for jj in range(CH):
+                    v_quant(t // 4 - 1, jj)
+            if t % 4 == 3 and t > 4:
+                contrast(t // 4 - 1, 0, ["o0", "o1", "o2", "o3"])
+            if t in (11, 12):
+                for pt in (2 * (t - 11), 2 * (t - 11) + 1):
+                    park(pt)
+            if t in (3, 7, 11):
+                weight_order(t // 4 + 1)
 
         g = G - 1
+        v_transpose(g, 0)
+        v_exit(g, 0)
+        v_transpose(g, 1)
+        v_exit(g, 1)
+        times_weight(UNITS - 1, 2)
         v_quant(g, 0)
+        times_weight(UNITS - 1, 3)
+        v_quant(g, 1)
+        contrast(2, 1, ["m0", "m1"], range(2), 2)
         v_transpose(g, 2)
         v_exit(g, 2)
-        v_quant(g, 1)
-        contrast(g, 0, None)
-        for gg in range(G - 1):
-            contrast(gg, 1, ["m0", "m1"], range(2))
         v_transpose(g, 3)
         v_exit(g, 3)
+        contrast(g, 0, None)
         v_quant(g, 2)
+        v_quant(g, 3)
         for pt in range(PT):
             store(0, pt)
-        for gg in range(G - 1):
-            contrast(gg, 1, [None, None, "o0", "o1"], range(2, PT))
-        v_quant(g, 3)
+        contrast(2, 1, [None, None, "o0", "o1"], range(2, PT), 2)
         contrast(g, 1, None)
         for pt in range(PT):
             store(1, pt)

@@ -23,6 +23,9 @@ G = M // 512
 NT = N // P
 PT = PF // P
 UNITS = M // 256
+PARKS = {(5, 1): ((0, 0), (0, 1)), (6, 0): ((0, 2), (0, 3)), (6, 1): ((1, 0), (1, 1)), (7, 1): ((1, 2), (1, 3))}
+VT_AT = {(2, 1): ((0, 0), (0, 1)), (3, 1): ((0, 2), (0, 3)), (4, 1): ((1, 0), (1, 1)), (5, 1): ((1, 2), (1, 3)), (6, 1): ((2, 0), (2, 1), (2, 2), (2, 3))}
+G2_AT = {(7, 0): (0, 1), (7, 1): (2, 3)}
 CH = 4
 
 
@@ -33,13 +36,13 @@ def tile_pca_residual_map_s13_kernel(
     with ExitStack() as ctx:
         keep = ctx.enter_context(tc.tile_pool(name="keep", bufs=1))
         xb_pool = ctx.enter_context(tc.tile_pool(name="xb_pool", bufs=8))
-        xg_pool = ctx.enter_context(tc.tile_pool(name="xg_pool", bufs=6))
+        xg_pool = ctx.enter_context(tc.tile_pool(name="xg_pool", bufs=3))
         cg_pool = ctx.enter_context(tc.tile_pool(name="cg_pool", bufs=3))
-        q_pool = ctx.enter_context(tc.tile_pool(name="q_pool", bufs=10))
-        vt_pool = ctx.enter_context(tc.tile_pool(name="vt_pool", bufs=8))
-        vg_pool = ctx.enter_context(tc.tile_pool(name="vg_pool", bufs=5))
-        res_pool = ctx.enter_context(tc.tile_pool(name="res_pool", bufs=8))
+        q_pool = ctx.enter_context(tc.tile_pool(name="q_pool", bufs=5))
+        vt_pool = ctx.enter_context(tc.tile_pool(name="vt_pool", bufs=4))
+        vg_pool = ctx.enter_context(tc.tile_pool(name="vg_pool", bufs=3))
         psum = ctx.enter_context(tc.psum_pool(name="psum", bufs=1))
+        ctx.enter_context(tc.manual_schedule(engines={mybir.EngineType.PE}))
 
         def bank(tag, dtype=F32):
             return psum.tile([P, 512 if dtype == F32 else 1024], dtype, name=tag)
@@ -63,7 +66,7 @@ def tile_pca_residual_map_s13_kernel(
             for h in range(2):
                 craw = keep.tile([P, 4, 512], BF16, name="craw%d%d" % (c, h))
                 c_raw[c, h] = craw
-        weight_bc = keep.tile([P, M], BF16, name="weight_bc")
+        weight_rows = keep.tile([P, 512], BF16, name="weight_rows")
         weight_upe = keep.tile([P, G, 2, 256], BF16, name="weight_upe")
         centre_rows = keep.tile([P, P], BF16, name="centre_rows")
         f_words = keep.tile([P, G, 2 * PF], U8, align_bytes=64, name="f_words")
@@ -72,6 +75,7 @@ def tile_pca_residual_map_s13_kernel(
         ident_bf = keep.tile([P, P], BF16, name="ident_bf")
         ident_f32 = keep.tile([P, P], F32, name="ident_f32")
         nc.gpsimd.memset(centre_rows[:], 0.0)
+        nc.gpsimd.memset(weight_rows[:], 0.0)
         make_identity(nc, ident_bf[:])
         make_identity(nc, ident_f32[:])
         nc.gpsimd.memset(f_scales[:].rearrange("p g n -> p (g n)").bitcast(I32), 0)
@@ -82,20 +86,14 @@ def tile_pca_residual_map_s13_kernel(
         def load_c(c, h):
             nc.sync.dma_start(out=c_raw[c, h][:], in_=c_rows[c][:, :, 512 * h : 512 * (h + 1)])
 
-        def load_w(g):
-            cols = slice(512 * g, 512 * (g + 1))
-            nc.sync.dma_start(out=weight_bc[:, cols], in_=weight[cols].partition_broadcast(P))
-
         load_x(0)
         nc.scalar.dma_start(out=centre_rows[0:NT, :], in_=centre.rearrange("(j p) -> j p", p=P))
+        nc.scalar.dma_start(out=weight_rows[0:G, :], in_=weight.rearrange("(g m) -> g m", g=G))
         for c in range(C):
             load_c(c, 0)
-        load_w(0)
         load_x(1)
         for c in range(C):
             load_c(c, 1)
-        for g in range(1, G):
-            load_w(g)
         load_x(2)
         load_x(3)
         nc.sync.dma_start(
@@ -135,7 +133,11 @@ def tile_pca_residual_map_s13_kernel(
 
         def next_t():
             counter["t"] += 1
-            return bank("t%d" % (counter["t"] % 2))
+            return bank("t%d" % (counter["t"] % 6))
+
+        def tail_t():
+            counter["t"] += 1
+            return bank("t%d" % (4 + counter["t"] % 2))
 
         def widen(r, pieces=1):
             xb = xb_pool.tile([P, K], BF16, name="xb")
@@ -159,27 +161,31 @@ def tile_pca_residual_map_s13_kernel(
                     nc.tensor.transpose(b[:, lo : lo + P], words[:, 256 * c + u : 256 * (c + 1) : 2], ident_f32[:])
 
         def x_exit(i, c):
-            xg = xg_pool.tile([P, 1024], BF16, align_bytes=64, name="xg")
-            xg_of[i, c] = xg
+            if c < 2:
+                xg = xg_pool.tile([P, 1024 * (c + 1)], BF16, align_bytes=64, name="xg%d" % c)
+                xg_of[i, c] = xg
+            part = xg_of[i, 0][:] if c == 0 else xg_of[i, 1][:, 1024 * (c - 1) : 1024 * c]
             nc.scalar.copy(
-                out=xg[:].bitcast(F32).rearrange("p (a r u) -> p a r u", a=2, u=2),
+                out=part.bitcast(F32).rearrange("p (a r u) -> p a r u", a=2, u=2),
                 in_=xbank_of[i, c][:].rearrange("p (a u r) -> p a r u", a=2, u=2),
             )
 
         def x_quant(i, c):
             if c == 0:
-                xc = xc_pool.tile([P, C, 256], U32, align_bytes=64, name="xc")
-                xs = xc_pool.tile([P, C, 256], U8, align_bytes=64, name="xs")
+                xc = xc_pool.tile([P, C * 256], U32, align_bytes=64, name="xc")
+                xs = xc_pool.tile([P, C * 256], U8, align_bytes=64, name="xs")
                 x_codes[i] = xc
                 x_scales[i] = xs
+            cols = slice(0, 256) if c == 0 else slice(256, 768)
             nc.vector.quantize_mx(
-                out=x_codes[i][:, c, :].bitcast(FP8X4), scales=x_scales[i][:, c, :], in_=xg_of[i, c][:]
+                out=x_codes[i][:, cols].bitcast(FP8X4), scales=x_scales[i][:, cols], in_=xg_of[i, c][:]
             )
+
 
         def c_interleave(c, h):
             for b in range(2):
                 counter["d"] += 1
-                bk = bank("o%d" % (counter["d"] % 4), BF16)
+                bk = bank("t%d" % (counter["d"] % 4), BF16)
                 cbank_of[c, h, b] = bk
                 for s in range(2):
                     n0 = 256 * b + 128 * s
@@ -214,193 +220,186 @@ def tile_pca_residual_map_s13_kernel(
                         out=b[:, 256 * s : 256 * (s + 1)],
                         lhsT=c_codes[:, c, cols].bitcast(FP8X4),
                         lhsT_scale=c_scales[:, c, cols],
-                        rhs=x_codes[i][:, c, :].bitcast(FP8X4),
-                        rhs_scale=x_scales[i][:, c, :],
+                        rhs=x_codes[i][:, 256 * c : 256 * (c + 1)].bitcast(FP8X4),
+                        rhs_scale=x_scales[i][:, 256 * c : 256 * (c + 1)],
                         start=(c == 0),
                         stop=(c == C - 1),
                     )
 
         def square(i, j):
-            qt = q_pool.tile([P, 512], F32, name="qt")
-            q_of[i, j] = qt
+            if j % 2 == 0:
+                qt = q_pool.tile([P, 4, 256], F32, name="qt")
+                q_of[i, j // 2] = qt
             for s in range(2):
                 nt = 2 * j + s
-                half = slice(256 * s, 256 * (s + 1))
                 nc.scalar.activation(
-                    out=qt[:, half].rearrange("n (u p e) -> n u p e", u=2, e=2),
-                    in_=m_of[i, j][:, half].rearrange("n (p u e) -> n u p e", u=2, e=2),
+                    out=q_of[i, j // 2][:, nt % 4].rearrange("n (u p e) -> n u p e", u=2, e=2),
+                    in_=m_of[i, j][:, 256 * s : 256 * (s + 1)].rearrange("n (p u e) -> n u p e", u=2, e=2),
                     func=ACT.Square,
                     bias=neg_centre[:, nt : nt + 1],
                     scale=1.0,
                 )
 
-        def weight_order(g):
+        def spread_weight(g):
+            b = bank(("m0", "m1", "t2", "t3")[g])
+            nc.tensor.matmul(
+                b[:], lhsT=ident_bf[:, g : g + 1].to_broadcast([P, P]), rhs=weight_rows[:], start=True, stop=True
+            )
             nc.scalar.copy(
                 out=weight_upe[:, g].rearrange("n u (p e) -> n u p e", e=2),
-                in_=weight_bc[:, 512 * g : 512 * (g + 1)].rearrange("n (p u e) -> n u p e", u=2, e=2),
+                in_=b[:].rearrange("n (p u e) -> n u p e", u=2, e=2),
             )
 
-        def times_weight(i, j):
+        def times_weight(i, half):
             g = i // 2
             lo = 128 * (i % 2)
             if i % 2 == 0:
-                vt = vt_pool.tile([P, 2, 2, 256], BF16, name="vt")
-                vt_of[g, j] = vt
-            w = weight_upe[:, g, :, lo : lo + 128]
+                vt = vt_pool.tile([P, 4, 2, 256], BF16, name="vt")
+                vt_of[g, half] = vt
             nc.vector.tensor_tensor(
-                out=vt_of[g, j][:, :, :, lo : lo + 128],
-                in0=q_of[i, j][:].rearrange("n (s u x) -> n s u x", s=2, u=2),
-                in1=w.unsqueeze(1).to_broadcast([P, 2, 2, 128]),
+                out=vt_of[g, half][:, :, :, lo : lo + 128],
+                in0=q_of[i, half][:].rearrange("n s (u x) -> n s u x", u=2),
+                in1=weight_upe[:, g, :, lo : lo + 128].unsqueeze(1).to_broadcast([P, 4, 2, 128]),
                 op=ALU.mult,
             )
 
         def v_transpose(g, j):
-            b = next_t()
+            b = next_t() if g < G - 1 else tail_t()
             vbank_of[g, j] = b
-            words = vt_of[g, j][:].rearrange("n s u x -> n (s u x)").bitcast(F32)
+            words = vt_of[g, j // 2][:].rearrange("n s u x -> n (s u x)").bitcast(F32)
             for s in range(4):
-                nc.tensor.transpose(b[:, P * s : P * (s + 1)], words[:, P * s : P * (s + 1)], ident_f32[:])
+                lo = 512 * (j % 2) + P * s
+                nc.tensor.transpose(b[:, P * s : P * (s + 1)], words[:, lo : lo + P], ident_f32[:])
 
         def v_exit(g, j):
-            vg = vg_pool.tile([P, 1024], BF16, align_bytes=64, name="vg")
-            vg_of[g, j] = vg
+            if j % 2 == 0:
+                vg = vg_pool.tile([P, 2048], BF16, align_bytes=64, name="vg")
+                vg_of[g, j // 2] = vg
             nc.scalar.copy(
-                out=vg[:].bitcast(F32).rearrange("p (a r u) -> p a r u", a=2, u=2),
+                out=vg_of[g, j // 2][:, 1024 * (j % 2) : 1024 * (j % 2) + 1024].bitcast(F32).rearrange("p (a r u) -> p a r u", a=2, u=2),
                 in_=vbank_of[g, j][:].rearrange("p (a u r) -> p a r u", a=2, u=2),
             )
 
         def v_quant(g, j):
-            cols = slice(256 * j, 256 * (j + 1))
+            cols = slice(512 * j, 512 * (j + 1))
             nc.vector.quantize_mx(
                 out=v_codes[:, g, cols].bitcast(FP8X4), scales=v_scales[:, g, cols], in_=vg_of[g, j][:]
             )
 
-        def contrast(g, h, tags, pts=range(PT), first=0):
-            for pt in pts:
-                if g == first:
-                    o_of[h, pt] = bank(tags[pt])
+        def contrast(b, gs, h, pt, first, last):
+            for g in gs:
                 nc.tensor.matmul_mx(
-                    out=o_of[h, pt][:],
+                    out=b[:],
                     lhsT=f_words[:, g, 2 * P * pt : 2 * P * (pt + 1)].bitcast(FP4X4),
                     lhsT_scale=f_scales[:, g, P * pt : P * (pt + 1)],
                     rhs=v_codes[:, g, 512 * h : 512 * (h + 1)].bitcast(FP8X4),
                     rhs_scale=v_scales[:, g, 512 * h : 512 * (h + 1)],
                     start=(g == first),
-                    stop=(g == G - 1),
+                    stop=(g == last),
                 )
 
-        def park(pt):
-            b = next_t()
-            for g in range(2):
-                nc.tensor.matmul_mx(
-                    out=b[:],
-                    lhsT=f_words[:, g, 2 * P * pt : 2 * P * (pt + 1)].bitcast(FP4X4),
-                    lhsT_scale=f_scales[:, g, P * pt : P * (pt + 1)],
-                    rhs=v_codes[:, g, 512:1024].bitcast(FP8X4),
-                    rhs_scale=v_scales[:, g, 512:1024],
-                    start=(g == 0),
-                    stop=(g == 1),
-                )
-            part = keep.tile([P, 512], F32, name="part%d" % pt)
-            part_of[pt] = part
+        def park(h, pt, gs):
+            b = next_t() if gs[-1] == 1 else tail_t()
+            contrast(b, gs, h, pt, gs[0], gs[-1])
+            part = keep.tile([P, 512], F32, name="part%d%d" % (h, pt))
+            part_of[h, pt] = part
             nc.scalar.copy(out=part[:], in_=b[:])
 
         def store(h, pt):
-            res = res_pool.tile([P, 512], F32, name="res")
-            if h == 1:
-                nc.vector.tensor_tensor(out=res[:], in0=o_of[h, pt][:], in1=part_of[pt][:], op=ALU.add)
-            elif pt % 2 == 0:
-                nc.scalar.copy(out=res[:], in_=o_of[h, pt][:])
-            else:
-                nc.vector.tensor_copy(out=res[:], in_=o_of[h, pt][:])
-            nc.sync.dma_start(out=out[P * pt : P * (pt + 1), 512 * h : 512 * (h + 1)], in_=res[:])
+            part = part_of[h, pt]
+            nc.vector.tensor_tensor(out=part[:], in0=o_of[h, pt][:], in1=part[:], op=ALU.add)
+            nc.sync.dma_start(out=out[P * pt : P * (pt + 1), 512 * h : 512 * (h + 1)], in_=part[:])
 
         widen(0, 3)
         widen(1, 3)
+        centre_bank = bank("t4", BF16)
+        nc.tensor.transpose(centre_bank[:, 0:P], centre_rows[:], ident_bf[:])
+        nc.scalar.activation(out=neg_centre[:], in_=centre_bank[:, 0:NT], func=ACT.Copy, scale=-1.0)
+        for g in range(G):
+            spread_weight(g)
         c_interleave(0, 0)
         c_exit(0, 0)
-        c_interleave(1, 0)
         x_transpose(0, 0)
         x_exit(0, 0)
-        c_exit(1, 0)
         x_transpose(0, 1)
         x_exit(0, 1)
+        c_interleave(1, 0)
+        c_exit(1, 0)
         x_transpose(0, 2)
         x_exit(0, 2)
         c_interleave(2, 0)
         c_exit(2, 0)
-        widen(2)
         c_quant(0, 0)
         x_quant(0, 0)
         c_quant(1, 0)
         x_quant(0, 1)
-        x_quant(0, 2)
         c_quant(2, 0)
-        centre_bank = bank("m0", BF16)
-        nc.tensor.transpose(centre_bank[:, 0:P], centre_rows[:], ident_bf[:])
-        nc.scalar.activation(out=neg_centre[:], in_=centre_bank[:, 0:NT], func=ACT.Copy, scale=-1.0)
-        weight_order(0)
-        widen(3)
+        widen(2, 1)
+        widen(3, 1)
+        c_interleave(0, 1)
+        c_exit(0, 1)
+        c_quant(0, 1)
+        c_interleave(1, 1)
+        c_exit(1, 1)
+        c_quant(1, 1)
+        widen(4)
 
-        GROUPS = 2 * UNITS
-        for t in range(GROUPS):
-            i, b = t // 2, t % 2
-            for j in (2 * b, 2 * b + 1):
-                mm(i, j)
-                square(i, j)
-            if t == 0:
-                for c in range(C):
-                    c_interleave(c, 1)
-                    c_exit(c, 1)
-                    c_quant(c, 1)
-            if t > 0:
-                times_weight((t - 1) // 2, 2 * ((t - 1) % 2))
-            if t + 4 < 2 * UNITS:
-                widen(t + 4)
-            if b == 0 and i + 1 < UNITS:
-                for c in range(C):
-                    x_transpose(i + 1, c)
-                    x_exit(i + 1, c)
-            if t > 0:
-                times_weight((t - 1) // 2, 2 * ((t - 1) % 2) + 1)
-            if b == 1 and i + 1 < UNITS:
-                for c in range(C):
-                    x_quant(i + 1, c)
-            if t % 4 == 1 and t > 4:
-                for jj in range(CH):
-                    v_transpose(t // 4 - 1, jj)
-                    v_exit(t // 4 - 1, jj)
-            if t % 4 == 2 and t > 4:
-                for jj in range(CH):
-                    v_quant(t // 4 - 1, jj)
-            if t % 4 == 3 and t > 4:
-                contrast(t // 4 - 1, 0, ["o0", "o1", "o2", "o3"])
-            if t in (11, 12):
-                for pt in (2 * (t - 11), 2 * (t - 11) + 1):
-                    park(pt)
-            if t in (3, 7, 11):
-                weight_order(t // 4 + 1)
+        for i in range(UNITS):
+            for half in range(2):
+                for j in (2 * half, 2 * half + 1):
+                    mm(i, j)
+                    square(i, j)
+                if i == 0 and half == 0:
+                    c_interleave(2, 1)
+                    c_exit(2, 1)
+                    c_quant(2, 1)
+                r = 2 * i + 5 + half
+                if r < 2 * UNITS:
+                    widen(r)
+                for h, pt in PARKS.get((i, half), ()):
+                    park(h, pt, (0, 1, 2) if i == 7 else (0, 1))
+                for pt in G2_AT.get((i, half), ()):
+                    b = bank("t%d" % pt)
+                    o_of[0, pt] = b
+                    contrast(b, (2,), 0, pt, 2, 3)
+                if half == 0:
+                    xs = [(i + 1, c) for c in ((0, 1, 2) if i == 0 else (1, 2))]
+                else:
+                    xs = [(i + 2, 0)]
+                for n, c in xs:
+                    if n < UNITS:
+                        x_transpose(n, c)
+                        x_exit(n, c)
+                        if c != 1:
+                            x_quant(n, c // 2)
+                for g, j in VT_AT.get((i, half), ()):
+                    v_transpose(g, j)
+                    v_exit(g, j)
+                    if j % 2 == 1:
+                        v_quant(g, j // 2)
+                times_weight(i, half)
 
         g = G - 1
         v_transpose(g, 0)
         v_exit(g, 0)
         v_transpose(g, 1)
         v_exit(g, 1)
-        times_weight(UNITS - 1, 2)
         v_quant(g, 0)
-        times_weight(UNITS - 1, 3)
-        v_quant(g, 1)
-        contrast(2, 1, ["m0", "m1"], range(2), 2)
+        for pt in range(2):
+            b = bank("m%d" % pt)
+            o_of[1, pt] = b
+            contrast(b, (2,), 1, pt, 2, 3)
         v_transpose(g, 2)
         v_exit(g, 2)
         v_transpose(g, 3)
         v_exit(g, 3)
-        contrast(g, 0, None)
-        v_quant(g, 2)
-        v_quant(g, 3)
+        v_quant(g, 1)
         for pt in range(PT):
+            contrast(o_of[0, pt], (3,), 0, pt, 2, 3)
             store(0, pt)
-        contrast(2, 1, [None, None, "o0", "o1"], range(2, PT), 2)
-        contrast(g, 1, None)
         for pt in range(PT):
+            if pt >= 2:
+                b = bank("t%d" % (pt - 2))
+                o_of[1, pt] = b
+            contrast(o_of[1, pt], (3,), 1, pt, 2 if pt < 2 else 3, 3)
             store(1, pt)

@@ -24,8 +24,8 @@ NT = N // P
 PT = PF // P
 UNITS = M // 256
 PARKS = {(5, 1): ((0, 0), (0, 1)), (6, 0): ((0, 2), (0, 3)), (6, 1): ((1, 0), (1, 1)), (7, 1): ((1, 2), (1, 3))}
-VT_AT = {(2, 1): ((0, 0), (0, 1)), (3, 1): ((0, 2), (0, 3)), (4, 1): ((1, 0), (1, 1)), (5, 1): ((1, 2), (1, 3)), (6, 1): ((2, 0), (2, 1), (2, 2), (2, 3))}
-G2_AT = {(7, 0): (0, 1), (7, 1): (2, 3)}
+VT_AT = {(2, 1): ((0, 0), (0, 1)), (3, 1): ((0, 2), (0, 3)), (4, 1): ((1, 0), (1, 1)), (5, 1): ((1, 2), (1, 3)), (6, 1): ((2, 0), (2, 1)), (7, 0): ((2, 2), (2, 3))}
+G2_AT = {(7, 1): (0, 1, 2, 3)}
 CH = 4
 
 
@@ -35,7 +35,7 @@ def tile_pca_residual_map_s13_kernel(
     nc = tc.nc
     with ExitStack() as ctx:
         keep = ctx.enter_context(tc.tile_pool(name="keep", bufs=1))
-        xb_pool = ctx.enter_context(tc.tile_pool(name="xb_pool", bufs=8))
+        xb_pool = ctx.enter_context(tc.tile_pool(name="xb_pool", bufs=6))
         xg_pool = ctx.enter_context(tc.tile_pool(name="xg_pool", bufs=3))
         cg_pool = ctx.enter_context(tc.tile_pool(name="cg_pool", bufs=3))
         q_pool = ctx.enter_context(tc.tile_pool(name="q_pool", bufs=5))
@@ -48,9 +48,10 @@ def tile_pca_residual_map_s13_kernel(
             return psum.tile([P, 512 if dtype == F32 else 1024], dtype, name=tag)
 
         scale_bc = keep.tile([P, K], F32, name="scale_bc")
-        for c in range(C):
+
+        def load_scale(c):
             cols = slice(512 * c, 512 * (c + 1))
-            nc.scalar.dma_start(
+            nc.sync.dma_start(
                 out=scale_bc[:, cols],
                 in_=patches_scale[:, cols].rearrange("o k -> (o k)").partition_broadcast(P),
             )
@@ -86,7 +87,10 @@ def tile_pca_residual_map_s13_kernel(
         def load_c(c, h):
             nc.sync.dma_start(out=c_raw[c, h][:], in_=c_rows[c][:, :, 512 * h : 512 * (h + 1)])
 
+        load_scale(0)
         load_x(0)
+        load_scale(1)
+        load_scale(2)
         nc.scalar.dma_start(out=centre_rows[0:NT, :], in_=centre.rearrange("(j p) -> j p", p=P))
         nc.scalar.dma_start(out=weight_rows[0:G, :], in_=weight.rearrange("(g m) -> g m", g=G))
         for c in range(C):
@@ -96,6 +100,8 @@ def tile_pca_residual_map_s13_kernel(
             load_c(c, 1)
         load_x(2)
         load_x(3)
+        for i in range(4, UNITS):
+            load_x(i)
         nc.sync.dma_start(
             out=f_words[:].bitcast(I32), in_=filt_words.bitcast(I32).rearrange("g p x -> p g x")
         )
@@ -105,8 +111,6 @@ def tile_pca_residual_map_s13_kernel(
                 out=f_scales[32 * quad : 32 * quad + 4, :, :].bitcast(I32),
                 in_=f_scale_rows[4 * quad : 4 * quad + 4],
             )
-        for i in range(4, UNITS):
-            load_x(i)
 
         c_codes = keep.tile([P, C, N], U32, align_bytes=64, name="c_codes")
         c_scales = keep.tile([P, C, N], U8, align_bytes=64, name="c_scales")
@@ -121,7 +125,6 @@ def tile_pca_residual_map_s13_kernel(
         x_codes = {}
         x_scales = {}
         cg_of = {}
-        cbank_of = {}
         m_of = {}
         q_of = {}
         vt_of = {}
@@ -129,27 +132,31 @@ def tile_pca_residual_map_s13_kernel(
         vg_of = {}
         o_of = {}
         part_of = {}
-        counter = {"t": 0, "d": 0, "m": 0}
+        counter = {"t": 0, "m": 0}
 
-        def next_t():
+        def next_t(dtype=F32):
             counter["t"] += 1
-            return bank("t%d" % (counter["t"] % 6))
+            return bank("t%d" % (counter["t"] % 6), dtype)
 
         def tail_t():
             counter["t"] += 1
             return bank("t%d" % (4 + counter["t"] % 2))
 
-        def widen(r, pieces=1):
+        def widen_part(r, c):
+            if c == 0:
+                xb = xb_pool.tile([P, K], BF16, name="xb")
+                xb_of[r] = xb
+            cols = slice(512 * c, 512 * (c + 1))
+            nc.vector.tensor_tensor(
+                out=xb_of[r][:, cols], in0=x_bytes[r // 2][:, r % 2, cols].bitcast(F8), in1=scale_bc[:, cols], op=ALU.mult
+            )
+
+        def widen(r):
             xb = xb_pool.tile([P, K], BF16, name="xb")
             xb_of[r] = xb
-            w = K // pieces
-            for s in range(pieces):
-                nc.vector.tensor_tensor(
-                    out=xb[:, w * s : w * (s + 1)],
-                    in0=x_bytes[r // 2][:, r % 2, w * s : w * (s + 1)].bitcast(F8),
-                    in1=scale_bc[:, w * s : w * (s + 1)],
-                    op=ALU.mult,
-                )
+            nc.vector.tensor_tensor(
+                out=xb[:], in0=x_bytes[r // 2][:, r % 2, :].bitcast(F8), in1=scale_bc[:], op=ALU.mult
+            )
 
         def x_transpose(i, c):
             b = next_t()
@@ -182,26 +189,17 @@ def tile_pca_residual_map_s13_kernel(
             )
 
 
-        def c_interleave(c, h):
-            for b in range(2):
-                counter["d"] += 1
-                bk = bank("t%d" % (counter["d"] % 4), BF16)
-                cbank_of[c, h, b] = bk
-                for s in range(2):
-                    n0 = 256 * b + 128 * s
-                    nc.tensor.matmul(
-                        bk[:, 512 * s : 512 * (s + 1)],
-                        lhsT=ident_bf[:],
-                        rhs=c_raw[c, h][:, :, n0 : n0 + P].rearrange("p t n -> p n t"),
-                        start=True,
-                        stop=True,
-                    )
-
-        def c_exit(c, h):
+        def c_copy(c, h, on_vector=False):
             cg = cg_pool.tile([P, 2048], BF16, align_bytes=64, name="cg")
             cg_of[c, h] = cg
-            for b in range(2):
-                nc.scalar.copy(out=cg[:, 1024 * b : 1024 * (b + 1)], in_=cbank_of[c, h, b][:])
+            for b in range(1 if on_vector else 2):
+                w = 512 if on_vector else 256
+                dst = cg[:, 4 * w * b : 4 * w * (b + 1)].rearrange("p (n i t) -> p n t i", i=4, t=4)
+                src = c_raw[c, h][:, :, w * b : w * (b + 1)].rearrange("p t (n i) -> p n t i", i=4)
+                if on_vector:
+                    nc.vector.tensor_copy(out=dst, in_=src)
+                else:
+                    nc.scalar.copy(out=dst, in_=src)
 
         def c_quant(c, h):
             cols = slice(512 * h, 512 * (h + 1))
@@ -241,7 +239,7 @@ def tile_pca_residual_map_s13_kernel(
                 )
 
         def spread_weight(g):
-            b = bank(("m0", "m1", "t2", "t3")[g])
+            b = next_t()
             nc.tensor.matmul(
                 b[:], lhsT=ident_bf[:, g : g + 1].to_broadcast([P, P]), rhs=weight_rows[:], start=True, stop=True
             )
@@ -310,38 +308,36 @@ def tile_pca_residual_map_s13_kernel(
             nc.vector.tensor_tensor(out=part[:], in0=o_of[h, pt][:], in1=part[:], op=ALU.add)
             nc.sync.dma_start(out=out[P * pt : P * (pt + 1), 512 * h : 512 * (h + 1)], in_=part[:])
 
-        widen(0, 3)
-        widen(1, 3)
         centre_bank = bank("t4", BF16)
         nc.tensor.transpose(centre_bank[:, 0:P], centre_rows[:], ident_bf[:])
         nc.scalar.activation(out=neg_centre[:], in_=centre_bank[:, 0:NT], func=ACT.Copy, scale=-1.0)
         for g in range(G):
             spread_weight(g)
-        c_interleave(0, 0)
-        c_exit(0, 0)
+        for c in range(C):
+            for r in range(2):
+                widen_part(r, c)
         x_transpose(0, 0)
         x_exit(0, 0)
-        x_transpose(0, 1)
-        x_exit(0, 1)
-        c_interleave(1, 0)
-        c_exit(1, 0)
-        x_transpose(0, 2)
-        x_exit(0, 2)
-        c_interleave(2, 0)
-        c_exit(2, 0)
+        c_copy(0, 0, True)
         c_quant(0, 0)
         x_quant(0, 0)
+        c_copy(1, 0)
+        x_transpose(0, 1)
+        x_exit(0, 1)
+        x_transpose(0, 2)
+        x_exit(0, 2)
         c_quant(1, 0)
         x_quant(0, 1)
+        c_copy(2, 0)
         c_quant(2, 0)
-        widen(2, 1)
-        widen(3, 1)
-        c_interleave(0, 1)
-        c_exit(0, 1)
+        widen(2)
+        widen(3)
+        c_copy(0, 1)
         c_quant(0, 1)
-        c_interleave(1, 1)
-        c_exit(1, 1)
+        c_copy(1, 1)
         c_quant(1, 1)
+        c_copy(2, 1)
+        c_quant(2, 1)
         widen(4)
 
         for i in range(UNITS):
@@ -349,10 +345,6 @@ def tile_pca_residual_map_s13_kernel(
                 for j in (2 * half, 2 * half + 1):
                     mm(i, j)
                     square(i, j)
-                if i == 0 and half == 0:
-                    c_interleave(2, 1)
-                    c_exit(2, 1)
-                    c_quant(2, 1)
                 r = 2 * i + 5 + half
                 if r < 2 * UNITS:
                     widen(r)

@@ -3,30 +3,41 @@ from contextlib import ExitStack
 import concourse.mybir as mybir
 from concourse.masks import make_identity
 
-M, K, N, PF = 2048, 1536, 1024, 512
-FLOPS = 2 * M * K * N + 2 * M * N * PF
+M, K, N, FILTERS = 2048, 1536, 1024, 512
+FLOPS = 2 * M * K * N + 2 * M * N * FILTERS
 
 F32 = mybir.dt.float32
 BF16 = mybir.dt.bfloat16
 I32 = mybir.dt.int32
 U32 = mybir.dt.uint32
 U8 = mybir.dt.uint8
-F8 = mybir.dt.float8_e4m3fn
+FP8 = mybir.dt.float8_e4m3fn
 FP8X4 = mybir.dt.float8_e4m3fn_x4
 FP4X4 = mybir.dt.float4_e2m1fn_x4
 ACT = mybir.ActivationFunctionType
 ALU = mybir.AluOpType
 
 P = 128
-C = K // 512
-G = M // 512
-NT = N // P
-PT = PF // P
-UNITS = M // 256
-PARKS = {(5, 1): ((0, 0), (0, 1)), (6, 0): ((0, 2), (0, 3)), (6, 1): ((1, 0), (1, 1)), (7, 1): ((1, 2), (1, 3))}
-VT_AT = {(2, 1): ((0, 0), (0, 1)), (3, 1): ((0, 2), (0, 3)), (4, 1): ((1, 0), (1, 1)), (5, 1): ((1, 2), (1, 3)), (6, 1): ((2, 0), (2, 1)), (7, 0): ((2, 2), (2, 3))}
-G2_AT = {(7, 1): (0, 1, 2, 3)}
-CH = 4
+PACK = 4
+PASS = P * PACK
+HALF = 512
+SLAB = 256
+
+PASSES = K // PASS
+GROUPS = M // PASS
+SLABS = M // SLAB
+HALVES = N // HALF
+STEPS = SLABS * HALVES
+PAIRS = N // (2 * P)
+COMP_TILES = N // P
+FILTER_TILES = FILTERS // P
+
+LOOK_AHEAD = 5
+WEIGHT_LAG = 4
+TURNED_AT = {9: ((0, 0), (0, 1)), 11: ((0, 2), (0, 3)), 12: ((1, 0), (1, 1)), 13: ((1, 2), (1, 3))}
+FIRST_CONTRAST = STEPS - 2
+ROTATING = 6
+EARLY = 6
 
 
 def tile_pca_residual_map_s13_kernel(
@@ -35,363 +46,356 @@ def tile_pca_residual_map_s13_kernel(
     nc = tc.nc
     with ExitStack() as ctx:
         keep = ctx.enter_context(tc.tile_pool(name="keep", bufs=1))
-        xb_pool = ctx.enter_context(tc.tile_pool(name="xb_pool", bufs=6))
-        xg_pool = ctx.enter_context(tc.tile_pool(name="xg_pool", bufs=3))
-        cg_pool = ctx.enter_context(tc.tile_pool(name="cg_pool", bufs=3))
-        q_pool = ctx.enter_context(tc.tile_pool(name="q_pool", bufs=5))
-        vt_pool = ctx.enter_context(tc.tile_pool(name="vt_pool", bufs=4))
-        vg_pool = ctx.enter_context(tc.tile_pool(name="vg_pool", bufs=3))
+        row_pool = ctx.enter_context(tc.tile_pool(name="row_pool", bufs=8))
+        patch_pool = ctx.enter_context(tc.tile_pool(name="patch_pool", bufs=3))
+        comp_pool = ctx.enter_context(tc.tile_pool(name="comp_pool", bufs=3))
+        square_pool = ctx.enter_context(tc.tile_pool(name="square_pool", bufs=6))
+        value_pool = ctx.enter_context(tc.tile_pool(name="value_pool", bufs=5))
+        turned_pool = ctx.enter_context(tc.tile_pool(name="turned_pool", bufs=3))
+        code_pool = ctx.enter_context(tc.tile_pool(name="code_pool", bufs=3))
         psum = ctx.enter_context(tc.psum_pool(name="psum", bufs=1))
         ctx.enter_context(tc.manual_schedule(engines={mybir.EngineType.PE}))
 
-        def bank(tag, dtype=F32):
-            return psum.tile([P, 512 if dtype == F32 else 1024], dtype, name=tag)
+        banks_given = {"turned": 0, "product": 0}
 
-        scale_bc = keep.tile([P, K], F32, name="scale_bc")
+        def bank(tag):
+            return psum.tile([P, 512], F32, name=tag)
 
-        def load_scale(c):
-            cols = slice(512 * c, 512 * (c + 1))
-            nc.sync.dma_start(
-                out=scale_bc[:, cols],
-                in_=patches_scale[:, cols].rearrange("o k -> (o k)").partition_broadcast(P),
-            )
+        def turned_bank():
+            banks_given["turned"] += 1
+            return bank("t%d" % (banks_given["turned"] % ROTATING))
 
-        x_rows = patches_bytes.rearrange("(i a p) k -> i p a k", a=2, p=P)
-        x_bytes = []
-        for i in range(UNITS):
-            xby = keep.tile([P, 2, K], U8, name="xby%d" % i)
-            x_bytes.append(xby)
-        c_rows = comps.rearrange("(c p t) n -> c p t n", p=P, t=4)
-        c_raw = {}
-        for c in range(C):
-            for h in range(2):
-                craw = keep.tile([P, 4, 512], BF16, name="craw%d%d" % (c, h))
-                c_raw[c, h] = craw
-        weight_rows = keep.tile([P, 512], BF16, name="weight_rows")
-        weight_upe = keep.tile([P, G, 2, 256], BF16, name="weight_upe")
+        def product_bank():
+            banks_given["product"] += 1
+            return bank("m%d" % (banks_given["product"] % 2))
+
+        scale_rows = keep.tile([P, K], F32, name="scale_rows")
+        slab_bytes = []
+        for i in range(SLABS):
+            bytes_tile = keep.tile([P, 2, K], U8, name="slab_bytes%d" % i)
+            slab_bytes.append(bytes_tile)
+        raw = {}
+        for c in range(PASSES):
+            for h in range(HALVES):
+                raw_tile = keep.tile([P, PACK, HALF], BF16, name="raw%d%d" % (c, h))
+                raw[c, h] = raw_tile
+        weight_rows = keep.tile([P, PASS], BF16, name="weight_rows")
         centre_rows = keep.tile([P, P], BF16, name="centre_rows")
-        f_words = keep.tile([P, G, 2 * PF], U8, align_bytes=64, name="f_words")
-        f_scales = keep.tile([P, G, PF], U8, align_bytes=64, name="f_scales")
+        filter_words = keep.tile([P, GROUPS, 2 * FILTERS], U8, align_bytes=64, name="filter_words")
+        filter_scales = keep.tile([P, GROUPS, FILTERS], U8, align_bytes=64, name="filter_scales")
 
-        ident_bf = keep.tile([P, P], BF16, name="ident_bf")
+        ident_bf16 = keep.tile([P, P], BF16, name="ident_bf16")
         ident_f32 = keep.tile([P, P], F32, name="ident_f32")
         nc.gpsimd.memset(centre_rows[:], 0.0)
         nc.gpsimd.memset(weight_rows[:], 0.0)
-        make_identity(nc, ident_bf[:])
+        make_identity(nc, ident_bf16[:])
         make_identity(nc, ident_f32[:])
-        nc.gpsimd.memset(f_scales[:].rearrange("p g n -> p (g n)").bitcast(I32), 0)
+        nc.gpsimd.memset(filter_scales[:].rearrange("p g n -> p (g n)").bitcast(I32), 0)
 
-        def load_x(i):
-            nc.sync.dma_start(out=x_bytes[i][:], in_=x_rows[i])
+        slab_rows = patches_bytes.rearrange("(i a p) k -> i p a k", a=2, p=P)
+        comp_rows = comps.rearrange("(c p t) n -> c p t n", p=P, t=PACK)
 
-        def load_c(c, h):
-            nc.sync.dma_start(out=c_raw[c, h][:], in_=c_rows[c][:, :, 512 * h : 512 * (h + 1)])
+        def load_scale(c):
+            cols = slice(PASS * c, PASS * (c + 1))
+            nc.sync.dma_start(
+                out=scale_rows[:, cols],
+                in_=patches_scale[:, cols].rearrange("o k -> (o k)").partition_broadcast(P),
+            )
+
+        def load_slab(i):
+            nc.sync.dma_start(out=slab_bytes[i][:], in_=slab_rows[i])
+
+        def load_comps(h):
+            for c in range(PASSES):
+                nc.sync.dma_start(out=raw[c, h][:], in_=comp_rows[c][:, :, HALF * h : HALF * (h + 1)])
 
         load_scale(0)
-        load_x(0)
+        load_slab(0)
         load_scale(1)
         load_scale(2)
-        nc.scalar.dma_start(out=centre_rows[0:NT, :], in_=centre.rearrange("(j p) -> j p", p=P))
-        nc.scalar.dma_start(out=weight_rows[0:G, :], in_=weight.rearrange("(g m) -> g m", g=G))
-        for c in range(C):
-            load_c(c, 0)
-        load_x(1)
-        for c in range(C):
-            load_c(c, 1)
-        load_x(2)
-        load_x(3)
-        for i in range(4, UNITS):
-            load_x(i)
+        nc.scalar.dma_start(out=centre_rows[0:COMP_TILES, :], in_=centre.rearrange("(j p) -> j p", p=P))
+        nc.scalar.dma_start(out=weight_rows[0:GROUPS, :], in_=weight.rearrange("(g m) -> g m", g=GROUPS))
+        load_comps(0)
+        load_slab(1)
+        load_comps(1)
+        for i in range(2, SLABS):
+            load_slab(i)
         nc.sync.dma_start(
-            out=f_words[:].bitcast(I32), in_=filt_words.bitcast(I32).rearrange("g p x -> p g x")
+            out=filter_words[:].bitcast(I32), in_=filt_words.bitcast(I32).rearrange("g p x -> p g x")
         )
-        f_scale_rows = filt_scales.bitcast(I32).rearrange("g q n -> q g n")
-        for quad in range(4):
+        filter_scale_rows = filt_scales.bitcast(I32).rearrange("g q n -> q g n")
+        for q in range(4):
             nc.sync.dma_start(
-                out=f_scales[32 * quad : 32 * quad + 4, :, :].bitcast(I32),
-                in_=f_scale_rows[4 * quad : 4 * quad + 4],
+                out=filter_scales[32 * q : 32 * q + 4, :, :].bitcast(I32), in_=filter_scale_rows[4 * q : 4 * q + 4]
             )
 
-        c_codes = keep.tile([P, C, N], U32, align_bytes=64, name="c_codes")
-        c_scales = keep.tile([P, C, N], U8, align_bytes=64, name="c_scales")
-        xc_pool = ctx.enter_context(tc.tile_pool(name="xc_pool", bufs=2))
-        v_codes = keep.tile([P, G, N], U32, align_bytes=64, name="v_codes")
-        v_scales = keep.tile([P, G, N], U8, align_bytes=64, name="v_scales")
-        neg_centre = keep.tile([P, NT], F32, name="neg_centre")
+        comp_codes = keep.tile([P, PASSES, N], U32, align_bytes=64, name="comp_codes")
+        comp_scales = keep.tile([P, PASSES, N], U8, align_bytes=64, name="comp_scales")
+        value_codes = keep.tile([P, GROUPS, N], U32, align_bytes=64, name="value_codes")
+        value_scales = keep.tile([P, GROUPS, N], U8, align_bytes=64, name="value_scales")
+        neg_centre = keep.tile([P, COMP_TILES], F32, name="neg_centre")
+        weights = keep.tile([P, GROUPS, 2, 2 * P], BF16, name="weights")
 
-        xb_of = {}
-        xbank_of = {}
-        xg_of = {}
-        x_codes = {}
-        x_scales = {}
-        cg_of = {}
-        m_of = {}
-        q_of = {}
-        vt_of = {}
-        vbank_of = {}
-        vg_of = {}
-        o_of = {}
-        part_of = {}
-        counter = {"t": 0, "m": 0}
+        rows = {}
+        patches = {}
+        patch_codes = {}
+        patch_scales = {}
+        interleaved = {}
+        products = {}
+        squares = {}
+        values = {}
+        grouped_values = {}
+        accumulators = {}
 
-        def next_t(dtype=F32):
-            counter["t"] += 1
-            return bank("t%d" % (counter["t"] % 6), dtype)
-
-        def tail_t():
-            counter["t"] += 1
-            return bank("t%d" % (4 + counter["t"] % 2))
-
-        def widen_part(r, c):
-            if c == 0:
-                xb = xb_pool.tile([P, K], BF16, name="xb")
-                xb_of[r] = xb
-            cols = slice(512 * c, 512 * (c + 1))
+        def widen_columns(r, cols):
             nc.vector.tensor_tensor(
-                out=xb_of[r][:, cols], in0=x_bytes[r // 2][:, r % 2, cols].bitcast(F8), in1=scale_bc[:, cols], op=ALU.mult
-            )
-
-        def widen(r):
-            xb = xb_pool.tile([P, K], BF16, name="xb")
-            xb_of[r] = xb
-            nc.vector.tensor_tensor(
-                out=xb[:], in0=x_bytes[r // 2][:, r % 2, :].bitcast(F8), in1=scale_bc[:], op=ALU.mult
-            )
-
-        def x_transpose(i, c):
-            b = next_t()
-            xbank_of[i, c] = b
-            for a in range(2):
-                words = xb_of[2 * i + a][:].bitcast(F32)
-                for u in range(2):
-                    lo = 256 * a + 128 * u
-                    nc.tensor.transpose(b[:, lo : lo + P], words[:, 256 * c + u : 256 * (c + 1) : 2], ident_f32[:])
-
-        def x_exit(i, c):
-            if c < 2:
-                xg = xg_pool.tile([P, 1024 * (c + 1)], BF16, align_bytes=64, name="xg%d" % c)
-                xg_of[i, c] = xg
-            part = xg_of[i, 0][:] if c == 0 else xg_of[i, 1][:, 1024 * (c - 1) : 1024 * c]
-            nc.scalar.copy(
-                out=part.bitcast(F32).rearrange("p (a r u) -> p a r u", a=2, u=2),
-                in_=xbank_of[i, c][:].rearrange("p (a u r) -> p a r u", a=2, u=2),
-            )
-
-        def x_quant(i, c):
-            if c == 0:
-                xc = xc_pool.tile([P, C * 256], U32, align_bytes=64, name="xc")
-                xs = xc_pool.tile([P, C * 256], U8, align_bytes=64, name="xs")
-                x_codes[i] = xc
-                x_scales[i] = xs
-            cols = slice(0, 256) if c == 0 else slice(256, 768)
-            nc.vector.quantize_mx(
-                out=x_codes[i][:, cols].bitcast(FP8X4), scales=x_scales[i][:, cols], in_=xg_of[i, c][:]
-            )
-
-
-        def c_copy(c, h, on_vector=False):
-            cg = cg_pool.tile([P, 2048], BF16, align_bytes=64, name="cg")
-            cg_of[c, h] = cg
-            for b in range(1 if on_vector else 2):
-                w = 512 if on_vector else 256
-                dst = cg[:, 4 * w * b : 4 * w * (b + 1)].rearrange("p (n i t) -> p n t i", i=4, t=4)
-                src = c_raw[c, h][:, :, w * b : w * (b + 1)].rearrange("p t (n i) -> p n t i", i=4)
-                if on_vector:
-                    nc.vector.tensor_copy(out=dst, in_=src)
-                else:
-                    nc.scalar.copy(out=dst, in_=src)
-
-        def c_quant(c, h):
-            cols = slice(512 * h, 512 * (h + 1))
-            nc.vector.quantize_mx(
-                out=c_codes[:, c, cols].bitcast(FP8X4), scales=c_scales[:, c, cols], in_=cg_of[c, h][:]
-            )
-
-        def mm(i, j):
-            counter["m"] += 1
-            b = bank("m%d" % (counter["m"] % 2))
-            m_of[i, j] = b
-            for s in range(2):
-                cols = slice(P * (2 * j + s), P * (2 * j + s + 1))
-                for c in range(C):
-                    nc.tensor.matmul_mx(
-                        out=b[:, 256 * s : 256 * (s + 1)],
-                        lhsT=c_codes[:, c, cols].bitcast(FP8X4),
-                        lhsT_scale=c_scales[:, c, cols],
-                        rhs=x_codes[i][:, 256 * c : 256 * (c + 1)].bitcast(FP8X4),
-                        rhs_scale=x_scales[i][:, 256 * c : 256 * (c + 1)],
-                        start=(c == 0),
-                        stop=(c == C - 1),
-                    )
-
-        def square(i, j):
-            if j % 2 == 0:
-                qt = q_pool.tile([P, 4, 256], F32, name="qt")
-                q_of[i, j // 2] = qt
-            for s in range(2):
-                nt = 2 * j + s
-                nc.scalar.activation(
-                    out=q_of[i, j // 2][:, nt % 4].rearrange("n (u p e) -> n u p e", u=2, e=2),
-                    in_=m_of[i, j][:, 256 * s : 256 * (s + 1)].rearrange("n (p u e) -> n u p e", u=2, e=2),
-                    func=ACT.Square,
-                    bias=neg_centre[:, nt : nt + 1],
-                    scale=1.0,
-                )
-
-        def spread_weight(g):
-            b = next_t()
-            nc.tensor.matmul(
-                b[:], lhsT=ident_bf[:, g : g + 1].to_broadcast([P, P]), rhs=weight_rows[:], start=True, stop=True
-            )
-            nc.scalar.copy(
-                out=weight_upe[:, g].rearrange("n u (p e) -> n u p e", e=2),
-                in_=b[:].rearrange("n (p u e) -> n u p e", u=2, e=2),
-            )
-
-        def times_weight(i, half):
-            g = i // 2
-            lo = 128 * (i % 2)
-            if i % 2 == 0:
-                vt = vt_pool.tile([P, 4, 2, 256], BF16, name="vt")
-                vt_of[g, half] = vt
-            nc.vector.tensor_tensor(
-                out=vt_of[g, half][:, :, :, lo : lo + 128],
-                in0=q_of[i, half][:].rearrange("n s (u x) -> n s u x", u=2),
-                in1=weight_upe[:, g, :, lo : lo + 128].unsqueeze(1).to_broadcast([P, 4, 2, 128]),
+                out=rows[r][:, cols],
+                in0=slab_bytes[r // 2][:, r % 2, cols].bitcast(FP8),
+                in1=scale_rows[:, cols],
                 op=ALU.mult,
             )
 
-        def v_transpose(g, j):
-            b = next_t() if g < G - 1 else tail_t()
-            vbank_of[g, j] = b
-            words = vt_of[g, j // 2][:].rearrange("n s u x -> n (s u x)").bitcast(F32)
-            for s in range(4):
-                lo = 512 * (j % 2) + P * s
-                nc.tensor.transpose(b[:, P * s : P * (s + 1)], words[:, lo : lo + P], ident_f32[:])
+        def widen(r):
+            row = row_pool.tile([P, K], BF16, name="row")
+            rows[r] = row
+            widen_columns(r, slice(0, K))
 
-        def v_exit(g, j):
-            if j % 2 == 0:
-                vg = vg_pool.tile([P, 2048], BF16, align_bytes=64, name="vg")
-                vg_of[g, j // 2] = vg
+        def turn_patches(i, c):
+            b = turned_bank()
+            for a in range(2):
+                words = rows[2 * i + a][:].bitcast(F32)
+                for u in range(2):
+                    at = SLAB * a + P * u
+                    first = PASS // 2 * c
+                    nc.tensor.transpose(
+                        b[:, at : at + P], words[:, first + u : first + PASS // 2 : 2], ident_f32[:]
+                    )
+            if c < 2:
+                tile = patch_pool.tile([P, PACK * SLAB * (c + 1)], BF16, align_bytes=64, name="patches%d" % c)
+                patches[i, c] = tile
+            dst = patches[i, 0][:] if c == 0 else patches[i, 1][:, PACK * SLAB * (c - 1) : PACK * SLAB * c]
             nc.scalar.copy(
-                out=vg_of[g, j // 2][:, 1024 * (j % 2) : 1024 * (j % 2) + 1024].bitcast(F32).rearrange("p (a r u) -> p a r u", a=2, u=2),
-                in_=vbank_of[g, j][:].rearrange("p (a u r) -> p a r u", a=2, u=2),
+                out=dst.bitcast(F32).rearrange("p (a r u) -> p a r u", a=2, u=2),
+                in_=b[:].rearrange("p (a u r) -> p a r u", a=2, u=2),
             )
 
-        def v_quant(g, j):
-            cols = slice(512 * j, 512 * (j + 1))
+        def quantize_patches(i, part):
+            if part == 0:
+                codes = code_pool.tile([P, PASSES * SLAB], U32, align_bytes=64, name="codes")
+                scales = code_pool.tile([P, PASSES * SLAB], U8, align_bytes=64, name="scales")
+                patch_codes[i] = codes
+                patch_scales[i] = scales
+            cols = slice(0, SLAB) if part == 0 else slice(SLAB, PASSES * SLAB)
             nc.vector.quantize_mx(
-                out=v_codes[:, g, cols].bitcast(FP8X4), scales=v_scales[:, g, cols], in_=vg_of[g, j][:]
+                out=patch_codes[i][:, cols].bitcast(FP8X4), scales=patch_scales[i][:, cols], in_=patches[i, part][:]
             )
 
-        def contrast(b, gs, h, pt, first, last):
-            for g in gs:
-                nc.tensor.matmul_mx(
-                    out=b[:],
-                    lhsT=f_words[:, g, 2 * P * pt : 2 * P * (pt + 1)].bitcast(FP4X4),
-                    lhsT_scale=f_scales[:, g, P * pt : P * (pt + 1)],
-                    rhs=v_codes[:, g, 512 * h : 512 * (h + 1)].bitcast(FP8X4),
-                    rhs_scale=v_scales[:, g, 512 * h : 512 * (h + 1)],
-                    start=(g == first),
-                    stop=(g == last),
+        def interleave(c, h, copy, pieces):
+            tile = comp_pool.tile([P, PACK * HALF], BF16, align_bytes=64, name="interleaved")
+            interleaved[c, h] = tile
+            width = HALF // pieces
+            for s in range(pieces):
+                copy(
+                    out=tile[:, PACK * width * s : PACK * width * (s + 1)].rearrange(
+                        "p (n i t) -> p n t i", i=4, t=PACK
+                    ),
+                    in_=raw[c, h][:, :, width * s : width * (s + 1)].rearrange("p t (n i) -> p n t i", i=4),
                 )
 
-        def park(h, pt, gs):
-            b = next_t() if gs[-1] == 1 else tail_t()
-            contrast(b, gs, h, pt, gs[0], gs[-1])
-            part = keep.tile([P, 512], F32, name="part%d%d" % (h, pt))
-            part_of[h, pt] = part
-            nc.scalar.copy(out=part[:], in_=b[:])
+        def quantize_comps(c, h):
+            cols = slice(HALF * h, HALF * (h + 1))
+            nc.vector.quantize_mx(
+                out=comp_codes[:, c, cols].bitcast(FP8X4), scales=comp_scales[:, c, cols], in_=interleaved[c, h][:]
+            )
 
-        def store(h, pt):
-            part = part_of[h, pt]
-            nc.vector.tensor_tensor(out=part[:], in0=o_of[h, pt][:], in1=part[:], op=ALU.add)
-            nc.sync.dma_start(out=out[P * pt : P * (pt + 1), 512 * h : 512 * (h + 1)], in_=part[:])
+        def multiply(i, j):
+            b = product_bank()
+            products[i, j] = b
+            for s in range(2):
+                comp_cols = slice(P * (2 * j + s), P * (2 * j + s + 1))
+                for c in range(PASSES):
+                    patch_cols = slice(SLAB * c, SLAB * (c + 1))
+                    nc.tensor.matmul_mx(
+                        out=b[:, SLAB * s : SLAB * (s + 1)],
+                        lhsT=comp_codes[:, c, comp_cols].bitcast(FP8X4),
+                        lhsT_scale=comp_scales[:, c, comp_cols],
+                        rhs=patch_codes[i][:, patch_cols].bitcast(FP8X4),
+                        rhs_scale=patch_scales[i][:, patch_cols],
+                        start=(c == 0),
+                        stop=(c == PASSES - 1),
+                    )
 
-        centre_bank = bank("t4", BF16)
-        nc.tensor.transpose(centre_bank[:, 0:P], centre_rows[:], ident_bf[:])
-        nc.scalar.activation(out=neg_centre[:], in_=centre_bank[:, 0:NT], func=ACT.Copy, scale=-1.0)
-        for g in range(G):
-            spread_weight(g)
-        for c in range(C):
+        def square(i, j):
+            h = j // 2
+            if j % 2 == 0:
+                tile = square_pool.tile([P, 4, SLAB], F32, name="squares")
+                squares[i, h] = tile
+            for s in range(2):
+                comp_tile = 2 * j + s
+                nc.scalar.activation(
+                    out=squares[i, h][:, comp_tile % 4].rearrange("n (u p e) -> n u p e", u=2, e=2),
+                    in_=products[i, j][:, SLAB * s : SLAB * (s + 1)].rearrange("n (p u e) -> n u p e", u=2, e=2),
+                    func=ACT.Square,
+                    bias=neg_centre[:, comp_tile : comp_tile + 1],
+                    scale=1.0,
+                )
+
+        def spread_weights(g):
+            b = turned_bank()
+            nc.tensor.matmul(
+                b[:], lhsT=ident_bf16[:, g : g + 1].to_broadcast([P, P]), rhs=weight_rows[:], start=True, stop=True
+            )
+            nc.scalar.copy(
+                out=weights[:, g].rearrange("n u (p e) -> n u p e", e=2),
+                in_=b[:].rearrange("n (p u e) -> n u p e", u=2, e=2),
+            )
+
+        def times_weight(i, h):
+            g = i // 2
+            cols = slice(P * (i % 2), P * (i % 2 + 1))
+            if i % 2 == 0:
+                tile = value_pool.tile([P, 4, 2, 2 * P], BF16, name="values")
+                values[g, h] = tile
+            nc.vector.tensor_tensor(
+                out=values[g, h][:, :, :, cols],
+                in0=squares[i, h][:].rearrange("n s (u x) -> n s u x", u=2),
+                in1=weights[:, g, :, cols].unsqueeze(1).to_broadcast([P, 4, 2, P]),
+                op=ALU.mult,
+            )
+
+        def turn_values(g, j):
+            b = turned_bank() if g < 2 else product_bank()
+            h = j // 2
+            words = values[g, h][:].rearrange("n s u x -> n (s u x)").bitcast(F32)
+            for s in range(4):
+                at = 512 * (j % 2) + P * s
+                nc.tensor.transpose(b[:, P * s : P * (s + 1)], words[:, at : at + P], ident_f32[:])
+            if j % 2 == 0:
+                tile = turned_pool.tile([P, PACK * HALF], BF16, align_bytes=64, name="grouped")
+                grouped_values[g, h] = tile
+            dst = grouped_values[g, h][:, 1024 * (j % 2) : 1024 * (j % 2 + 1)]
+            nc.scalar.copy(
+                out=dst.bitcast(F32).rearrange("p (a n u) -> p a n u", a=2, u=2),
+                in_=b[:].rearrange("p (a u n) -> p a n u", a=2, u=2),
+            )
+
+        def quantize_values(g, h):
+            cols = slice(HALF * h, HALF * (h + 1))
+            nc.vector.quantize_mx(
+                out=value_codes[:, g, cols].bitcast(FP8X4), scales=value_scales[:, g, cols], in_=grouped_values[g, h][:]
+            )
+
+        def contrast(g, h, f):
+            if g == 0:
+                k = FILTER_TILES * h + f
+                b = bank("t%d" % k if k < EARLY else "m%d" % (k - EARLY))
+                accumulators[h, f] = b
+            cols = slice(HALF * h, HALF * (h + 1))
+            nc.tensor.matmul_mx(
+                out=accumulators[h, f][:],
+                lhsT=filter_words[:, g, 2 * P * f : 2 * P * (f + 1)].bitcast(FP4X4),
+                lhsT_scale=filter_scales[:, g, P * f : P * (f + 1)],
+                rhs=value_codes[:, g, cols].bitcast(FP8X4),
+                rhs_scale=value_scales[:, g, cols],
+                start=(g == 0),
+                stop=(g == GROUPS - 1),
+            )
+
+        def store(h, f):
+            k = FILTER_TILES * h + f
+            if k < PASSES * HALVES:
+                result = keep.tile([P, HALF], F32, name="raw%d%d" % divmod(k, HALVES))
+            else:
+                result = comp_pool.tile([P, HALF], F32, align_bytes=64, name="interleaved")
+            if f % 2 == 0:
+                nc.scalar.copy(out=result[:], in_=accumulators[h, f][:])
+            else:
+                nc.vector.tensor_copy(out=result[:], in_=accumulators[h, f][:])
+            nc.sync.dma_start(out=out[P * f : P * (f + 1), HALF * h : HALF * (h + 1)], in_=result[:])
+
+        centre_bank = psum.tile([P, 1024], BF16, name="t4")
+        nc.tensor.transpose(centre_bank[:, 0:P], centre_rows[:], ident_bf16[:])
+        nc.scalar.activation(out=neg_centre[:], in_=centre_bank[:, 0:COMP_TILES], func=ACT.Copy, scale=-1.0)
+        for g in range(GROUPS):
+            spread_weights(g)
+        for c in range(PASSES):
             for r in range(2):
-                widen_part(r, c)
-        x_transpose(0, 0)
-        x_exit(0, 0)
-        c_copy(0, 0, True)
-        c_quant(0, 0)
-        x_quant(0, 0)
-        c_copy(1, 0)
-        x_transpose(0, 1)
-        x_exit(0, 1)
-        x_transpose(0, 2)
-        x_exit(0, 2)
-        c_quant(1, 0)
-        x_quant(0, 1)
-        c_copy(2, 0)
-        c_quant(2, 0)
-        widen(2)
-        widen(3)
-        c_copy(0, 1)
-        c_quant(0, 1)
-        c_copy(1, 1)
-        c_quant(1, 1)
-        c_copy(2, 1)
-        c_quant(2, 1)
-        widen(4)
+                if c == 0:
+                    row = row_pool.tile([P, K], BF16, name="row")
+                    rows[r] = row
+                widen_columns(r, slice(PASS * c, PASS * (c + 1)))
+        turn_patches(0, 0)
+        interleave(0, 0, nc.vector.tensor_copy, 1)
+        quantize_comps(0, 0)
+        quantize_patches(0, 0)
+        interleave(1, 0, nc.scalar.copy, 2)
+        turn_patches(0, 1)
+        turn_patches(0, 2)
+        quantize_comps(1, 0)
+        quantize_patches(0, 1)
+        interleave(2, 0, nc.vector.tensor_copy, 1)
+        quantize_comps(2, 0)
+        for r in range(2, LOOK_AHEAD):
+            widen(r)
 
-        for i in range(UNITS):
-            for half in range(2):
-                for j in (2 * half, 2 * half + 1):
-                    mm(i, j)
-                    square(i, j)
-                r = 2 * i + 5 + half
-                if r < 2 * UNITS:
-                    widen(r)
-                for h, pt in PARKS.get((i, half), ()):
-                    park(h, pt, (0, 1, 2) if i == 7 else (0, 1))
-                for pt in G2_AT.get((i, half), ()):
-                    b = bank("t%d" % pt)
-                    o_of[0, pt] = b
-                    contrast(b, (2,), 0, pt, 2, 3)
-                if half == 0:
-                    xs = [(i + 1, c) for c in ((0, 1, 2) if i == 0 else (1, 2))]
-                else:
-                    xs = [(i + 2, 0)]
-                for n, c in xs:
-                    if n < UNITS:
-                        x_transpose(n, c)
-                        x_exit(n, c)
-                        if c != 1:
-                            x_quant(n, c // 2)
-                for g, j in VT_AT.get((i, half), ()):
-                    v_transpose(g, j)
-                    v_exit(g, j)
-                    if j % 2 == 1:
-                        v_quant(g, j // 2)
-                times_weight(i, half)
+        def slab_and_half(t):
+            return (t % 2, t // 2) if t < 4 else (t // 2, t % 2)
 
-        g = G - 1
-        v_transpose(g, 0)
-        v_exit(g, 0)
-        v_transpose(g, 1)
-        v_exit(g, 1)
-        v_quant(g, 0)
-        for pt in range(2):
-            b = bank("m%d" % pt)
-            o_of[1, pt] = b
-            contrast(b, (2,), 1, pt, 2, 3)
-        v_transpose(g, 2)
-        v_exit(g, 2)
-        v_transpose(g, 3)
-        v_exit(g, 3)
-        v_quant(g, 1)
-        for pt in range(PT):
-            contrast(o_of[0, pt], (3,), 0, pt, 2, 3)
-            store(0, pt)
-        for pt in range(PT):
-            if pt >= 2:
-                b = bank("t%d" % (pt - 2))
-                o_of[1, pt] = b
-            contrast(o_of[1, pt], (3,), 1, pt, 2 if pt < 2 else 3, 3)
-            store(1, pt)
+        for t in range(STEPS):
+            i, h = slab_and_half(t)
+            for j in (2 * h, 2 * h + 1):
+                multiply(i, j)
+                square(i, j)
+            if t + LOOK_AHEAD < 2 * SLABS:
+                widen(t + LOOK_AHEAD)
+            if t >= FIRST_CONTRAST:
+                each = EARLY // (STEPS - FIRST_CONTRAST)
+                for k in range(each * (t - FIRST_CONTRAST), each * (t - FIRST_CONTRAST + 1)):
+                    contrast(0, k // FILTER_TILES, k % FILTER_TILES)
+            if t % 2 == 1:
+                slab, passes = t // 2 + 2, (0,)
+            else:
+                slab, passes = t // 2 + 1, (0, 1, 2) if t == 0 else (1, 2)
+            if slab < SLABS:
+                for c in passes:
+                    turn_patches(slab, c)
+                    if c != 1:
+                        quantize_patches(slab, c // 2)
+            if t == 0:
+                for c in range(PASSES):
+                    interleave(c, 1, nc.scalar.copy, 2)
+                    quantize_comps(c, 1)
+            for g, j in TURNED_AT.get(t, ()):
+                turn_values(g, j)
+                if j % 2 == 1:
+                    quantize_values(g, j // 2)
+            if t >= WEIGHT_LAG:
+                times_weight(*slab_and_half(t - WEIGHT_LAG))
+
+        for t in range(STEPS - WEIGHT_LAG, STEPS):
+            times_weight(*slab_and_half(t))
+
+        def turn_half(g, h):
+            turn_values(g, 2 * h)
+            turn_values(g, 2 * h + 1)
+            quantize_values(g, h)
+
+        turn_half(2, 0)
+        for k in range(EARLY):
+            contrast(1, k // FILTER_TILES, k % FILTER_TILES)
+        turn_half(2, 1)
+        for f in range(2):
+            contrast(2, 0, f)
+        turn_half(3, 0)
+        for k in range(2, EARLY):
+            contrast(2, k // FILTER_TILES, k % FILTER_TILES)
+        turn_half(3, 1)
+        for f in range(FILTER_TILES):
+            contrast(3, 0, f)
+            store(0, f)
+        for f in range(EARLY - FILTER_TILES, FILTER_TILES):
+            for g in range(GROUPS - 1):
+                contrast(g, 1, f)
+        for f in range(FILTER_TILES):
+            contrast(3, 1, f)
+            store(1, f)

from contextlib import ExitStack

import concourse.mybir as mybir
from concourse.masks import make_identity

M, K, N, FILTERS = 2048, 1536, 1024, 512
FLOPS = 2 * M * K * N + 2 * M * N * FILTERS

F32 = mybir.dt.float32
BF16 = mybir.dt.bfloat16
I32 = mybir.dt.int32
U32 = mybir.dt.uint32
U8 = mybir.dt.uint8
FP8 = mybir.dt.float8_e4m3fn
FP8X4 = mybir.dt.float8_e4m3fn_x4
FP4X4 = mybir.dt.float4_e2m1fn_x4
ACT = mybir.ActivationFunctionType
ALU = mybir.AluOpType

P = 128
PACK = 4
PASS = P * PACK
HALF = 512
SLAB = 256

PASSES = K // PASS
GROUPS = M // PASS
SLABS = M // SLAB
HALVES = N // HALF
STEPS = SLABS * HALVES
PAIRS = N // (2 * P)
COMP_TILES = N // P
FILTER_TILES = FILTERS // P

LOOK_AHEAD = 5
WEIGHT_LAG = 4
TURNED_AT = {9: ((0, 0), (0, 1)), 11: ((0, 2), (0, 3)), 12: ((1, 0), (1, 1)), 13: ((1, 2), (1, 3))}
FIRST_CONTRAST = STEPS - 2
ROTATING = 6
EARLY = 6


def tile_pca_residual_map_s13_kernel(
    tc, patches_bytes, patches_scale, comps, centre, weight, filt_words, filt_scales, out
):
    nc = tc.nc
    with ExitStack() as ctx:
        keep = ctx.enter_context(tc.tile_pool(name="keep", bufs=1))
        row_pool = ctx.enter_context(tc.tile_pool(name="row_pool", bufs=8))
        patch_pool = ctx.enter_context(tc.tile_pool(name="patch_pool", bufs=3))
        comp_pool = ctx.enter_context(tc.tile_pool(name="comp_pool", bufs=3))
        square_pool = ctx.enter_context(tc.tile_pool(name="square_pool", bufs=6))
        value_pool = ctx.enter_context(tc.tile_pool(name="value_pool", bufs=5))
        turned_pool = ctx.enter_context(tc.tile_pool(name="turned_pool", bufs=3))
        code_pool = ctx.enter_context(tc.tile_pool(name="code_pool", bufs=3))
        psum = ctx.enter_context(tc.psum_pool(name="psum", bufs=1))
        ctx.enter_context(tc.manual_schedule(engines={mybir.EngineType.PE}))

        banks_given = {"turned": 0, "product": 0}

        def bank(tag):
            return psum.tile([P, 512], F32, name=tag)

        def turned_bank():
            banks_given["turned"] += 1
            return bank("t%d" % (banks_given["turned"] % ROTATING))

        def product_bank():
            banks_given["product"] += 1
            return bank("m%d" % (banks_given["product"] % 2))

        scale_rows = keep.tile([P, K], F32, name="scale_rows")
        slab_bytes = []
        for i in range(SLABS):
            bytes_tile = keep.tile([P, 2, K], U8, name="slab_bytes%d" % i)
            slab_bytes.append(bytes_tile)
        raw = {}
        for c in range(PASSES):
            for h in range(HALVES):
                raw_tile = keep.tile([P, PACK, HALF], BF16, name="raw%d%d" % (c, h))
                raw[c, h] = raw_tile
        weight_rows = keep.tile([P, PASS], BF16, name="weight_rows")
        centre_rows = keep.tile([P, P], BF16, name="centre_rows")
        filter_words = keep.tile([P, GROUPS, 2 * FILTERS], U8, align_bytes=64, name="filter_words")
        filter_scales = keep.tile([P, GROUPS, FILTERS], U8, align_bytes=64, name="filter_scales")

        ident_bf16 = keep.tile([P, P], BF16, name="ident_bf16")
        ident_f32 = keep.tile([P, P], F32, name="ident_f32")
        nc.gpsimd.memset(centre_rows[:], 0.0)
        nc.gpsimd.memset(weight_rows[:], 0.0)
        make_identity(nc, ident_bf16[:])
        make_identity(nc, ident_f32[:])
        nc.gpsimd.memset(filter_scales[:].rearrange("p g n -> p (g n)").bitcast(I32), 0)

        slab_rows = patches_bytes.rearrange("(i a p) k -> i p a k", a=2, p=P)
        comp_rows = comps.rearrange("(c p t) n -> c p t n", p=P, t=PACK)

        def load_scale(c):
            cols = slice(PASS * c, PASS * (c + 1))
            nc.sync.dma_start(
                out=scale_rows[:, cols],
                in_=patches_scale[:, cols].rearrange("o k -> (o k)").partition_broadcast(P),
            )

        def load_slab(i):
            nc.sync.dma_start(out=slab_bytes[i][:], in_=slab_rows[i])

        def load_comps(h):
            for c in range(PASSES):
                nc.sync.dma_start(out=raw[c, h][:], in_=comp_rows[c][:, :, HALF * h : HALF * (h + 1)])

        load_scale(0)
        load_slab(0)
        load_scale(1)
        load_scale(2)
        nc.scalar.dma_start(out=centre_rows[0:COMP_TILES, :], in_=centre.rearrange("(j p) -> j p", p=P))
        nc.scalar.dma_start(out=weight_rows[0:GROUPS, :], in_=weight.rearrange("(g m) -> g m", g=GROUPS))
        load_comps(0)
        load_slab(1)
        load_comps(1)
        for i in range(2, SLABS):
            load_slab(i)
        nc.sync.dma_start(
            out=filter_words[:].bitcast(I32), in_=filt_words.bitcast(I32).rearrange("g p x -> p g x")
        )
        filter_scale_rows = filt_scales.bitcast(I32).rearrange("g q n -> q g n")
        for q in range(4):
            nc.sync.dma_start(
                out=filter_scales[32 * q : 32 * q + 4, :, :].bitcast(I32), in_=filter_scale_rows[4 * q : 4 * q + 4]
            )

        comp_codes = keep.tile([P, PASSES, N], U32, align_bytes=64, name="comp_codes")
        comp_scales = keep.tile([P, PASSES, N], U8, align_bytes=64, name="comp_scales")
        value_codes = keep.tile([P, GROUPS, N], U32, align_bytes=64, name="value_codes")
        value_scales = keep.tile([P, GROUPS, N], U8, align_bytes=64, name="value_scales")
        neg_centre = keep.tile([P, COMP_TILES], F32, name="neg_centre")
        weights = keep.tile([P, GROUPS, 2, 2 * P], BF16, name="weights")

        rows = {}
        patches = {}
        patch_codes = {}
        patch_scales = {}
        interleaved = {}
        products = {}
        squares = {}
        values = {}
        grouped_values = {}
        accumulators = {}

        def widen_columns(r, cols):
            nc.vector.tensor_tensor(
                out=rows[r][:, cols],
                in0=slab_bytes[r // 2][:, r % 2, cols].bitcast(FP8),
                in1=scale_rows[:, cols],
                op=ALU.mult,
            )

        def widen(r):
            row = row_pool.tile([P, K], BF16, name="row")
            rows[r] = row
            widen_columns(r, slice(0, K))

        def turn_patches(i, c):
            b = turned_bank()
            for a in range(2):
                words = rows[2 * i + a][:].bitcast(F32)
                for u in range(2):
                    at = SLAB * a + P * u
                    first = PASS // 2 * c
                    nc.tensor.transpose(
                        b[:, at : at + P], words[:, first + u : first + PASS // 2 : 2], ident_f32[:]
                    )
            if c < 2:
                tile = patch_pool.tile([P, PACK * SLAB * (c + 1)], BF16, align_bytes=64, name="patches%d" % c)
                patches[i, c] = tile
            dst = patches[i, 0][:] if c == 0 else patches[i, 1][:, PACK * SLAB * (c - 1) : PACK * SLAB * c]
            nc.scalar.copy(
                out=dst.bitcast(F32).rearrange("p (a r u) -> p a r u", a=2, u=2),
                in_=b[:].rearrange("p (a u r) -> p a r u", a=2, u=2),
            )

        def quantize_patches(i, part):
            if part == 0:
                codes = code_pool.tile([P, PASSES * SLAB], U32, align_bytes=64, name="codes")
                scales = code_pool.tile([P, PASSES * SLAB], U8, align_bytes=64, name="scales")
                patch_codes[i] = codes
                patch_scales[i] = scales
            cols = slice(0, SLAB) if part == 0 else slice(SLAB, PASSES * SLAB)
            nc.vector.quantize_mx(
                out=patch_codes[i][:, cols].bitcast(FP8X4), scales=patch_scales[i][:, cols], in_=patches[i, part][:]
            )

        def interleave(c, h, copy, pieces):
            tile = comp_pool.tile([P, PACK * HALF], BF16, align_bytes=64, name="interleaved")
            interleaved[c, h] = tile
            width = HALF // pieces
            for s in range(pieces):
                copy(
                    out=tile[:, PACK * width * s : PACK * width * (s + 1)].rearrange(
                        "p (n i t) -> p n t i", i=4, t=PACK
                    ),
                    in_=raw[c, h][:, :, width * s : width * (s + 1)].rearrange("p t (n i) -> p n t i", i=4),
                )

        def quantize_comps(c, h):
            cols = slice(HALF * h, HALF * (h + 1))
            nc.vector.quantize_mx(
                out=comp_codes[:, c, cols].bitcast(FP8X4), scales=comp_scales[:, c, cols], in_=interleaved[c, h][:]
            )

        def multiply(i, j):
            b = product_bank()
            products[i, j] = b
            for s in range(2):
                comp_cols = slice(P * (2 * j + s), P * (2 * j + s + 1))
                for c in range(PASSES):
                    patch_cols = slice(SLAB * c, SLAB * (c + 1))
                    nc.tensor.matmul_mx(
                        out=b[:, SLAB * s : SLAB * (s + 1)],
                        lhsT=comp_codes[:, c, comp_cols].bitcast(FP8X4),
                        lhsT_scale=comp_scales[:, c, comp_cols],
                        rhs=patch_codes[i][:, patch_cols].bitcast(FP8X4),
                        rhs_scale=patch_scales[i][:, patch_cols],
                        start=(c == 0),
                        stop=(c == PASSES - 1),
                    )

        def square(i, j):
            h = j // 2
            if j % 2 == 0:
                tile = square_pool.tile([P, 4, SLAB], F32, name="squares")
                squares[i, h] = tile
            for s in range(2):
                comp_tile = 2 * j + s
                nc.scalar.activation(
                    out=squares[i, h][:, comp_tile % 4].rearrange("n (u p e) -> n u p e", u=2, e=2),
                    in_=products[i, j][:, SLAB * s : SLAB * (s + 1)].rearrange("n (p u e) -> n u p e", u=2, e=2),
                    func=ACT.Square,
                    bias=neg_centre[:, comp_tile : comp_tile + 1],
                    scale=1.0,
                )

        def spread_weights(g):
            b = turned_bank()
            nc.tensor.matmul(
                b[:], lhsT=ident_bf16[:, g : g + 1].to_broadcast([P, P]), rhs=weight_rows[:], start=True, stop=True
            )
            nc.scalar.copy(
                out=weights[:, g].rearrange("n u (p e) -> n u p e", e=2),
                in_=b[:].rearrange("n (p u e) -> n u p e", u=2, e=2),
            )

        def times_weight(i, h):
            g = i // 2
            cols = slice(P * (i % 2), P * (i % 2 + 1))
            if i % 2 == 0:
                tile = value_pool.tile([P, 4, 2, 2 * P], BF16, name="values")
                values[g, h] = tile
            nc.vector.tensor_tensor(
                out=values[g, h][:, :, :, cols],
                in0=squares[i, h][:].rearrange("n s (u x) -> n s u x", u=2),
                in1=weights[:, g, :, cols].unsqueeze(1).to_broadcast([P, 4, 2, P]),
                op=ALU.mult,
            )

        def turn_values(g, j):
            b = turned_bank() if g < 2 else product_bank()
            h = j // 2
            words = values[g, h][:].rearrange("n s u x -> n (s u x)").bitcast(F32)
            for s in range(4):
                at = 512 * (j % 2) + P * s
                nc.tensor.transpose(b[:, P * s : P * (s + 1)], words[:, at : at + P], ident_f32[:])
            if j % 2 == 0:
                tile = turned_pool.tile([P, PACK * HALF], BF16, align_bytes=64, name="grouped")
                grouped_values[g, h] = tile
            dst = grouped_values[g, h][:, 1024 * (j % 2) : 1024 * (j % 2 + 1)]
            nc.scalar.copy(
                out=dst.bitcast(F32).rearrange("p (a n u) -> p a n u", a=2, u=2),
                in_=b[:].rearrange("p (a u n) -> p a n u", a=2, u=2),
            )

        def quantize_values(g, h):
            cols = slice(HALF * h, HALF * (h + 1))
            nc.vector.quantize_mx(
                out=value_codes[:, g, cols].bitcast(FP8X4), scales=value_scales[:, g, cols], in_=grouped_values[g, h][:]
            )

        def contrast(g, h, f):
            if g == 0:
                k = FILTER_TILES * h + f
                b = bank("t%d" % k if k < EARLY else "m%d" % (k - EARLY))
                accumulators[h, f] = b
            cols = slice(HALF * h, HALF * (h + 1))
            nc.tensor.matmul_mx(
                out=accumulators[h, f][:],
                lhsT=filter_words[:, g, 2 * P * f : 2 * P * (f + 1)].bitcast(FP4X4),
                lhsT_scale=filter_scales[:, g, P * f : P * (f + 1)],
                rhs=value_codes[:, g, cols].bitcast(FP8X4),
                rhs_scale=value_scales[:, g, cols],
                start=(g == 0),
                stop=(g == GROUPS - 1),
            )

        def store(h, f):
            k = FILTER_TILES * h + f
            if k < PASSES * HALVES:
                result = keep.tile([P, HALF], F32, name="raw%d%d" % divmod(k, HALVES))
            else:
                result = comp_pool.tile([P, HALF], F32, align_bytes=64, name="interleaved")
            if f % 2 == 0:
                nc.scalar.copy(out=result[:], in_=accumulators[h, f][:])
            else:
                nc.vector.tensor_copy(out=result[:], in_=accumulators[h, f][:])
            nc.sync.dma_start(out=out[P * f : P * (f + 1), HALF * h : HALF * (h + 1)], in_=result[:])

        centre_bank = psum.tile([P, 1024], BF16, name="t4")
        nc.tensor.transpose(centre_bank[:, 0:P], centre_rows[:], ident_bf16[:])
        nc.scalar.activation(out=neg_centre[:], in_=centre_bank[:, 0:COMP_TILES], func=ACT.Copy, scale=-1.0)
        for g in range(GROUPS):
            spread_weights(g)
        for c in range(PASSES):
            for r in range(2):
                if c == 0:
                    row = row_pool.tile([P, K], BF16, name="row")
                    rows[r] = row
                widen_columns(r, slice(PASS * c, PASS * (c + 1)))
        turn_patches(0, 0)
        interleave(0, 0, nc.vector.tensor_copy, 1)
        quantize_comps(0, 0)
        quantize_patches(0, 0)
        interleave(1, 0, nc.scalar.copy, 2)
        turn_patches(0, 1)
        turn_patches(0, 2)
        quantize_comps(1, 0)
        quantize_patches(0, 1)
        interleave(2, 0, nc.vector.tensor_copy, 1)
        quantize_comps(2, 0)
        for r in range(2, LOOK_AHEAD):
            widen(r)

        def slab_and_half(t):
            return (t % 2, t // 2) if t < 4 else (t // 2, t % 2)

        for t in range(STEPS):
            i, h = slab_and_half(t)
            for j in (2 * h, 2 * h + 1):
                multiply(i, j)
                square(i, j)
            if t + LOOK_AHEAD < 2 * SLABS:
                widen(t + LOOK_AHEAD)
            if t >= FIRST_CONTRAST:
                each = EARLY // (STEPS - FIRST_CONTRAST)
                for k in range(each * (t - FIRST_CONTRAST), each * (t - FIRST_CONTRAST + 1)):
                    contrast(0, k // FILTER_TILES, k % FILTER_TILES)
            if t % 2 == 1:
                slab, passes = t // 2 + 2, (0,)
            else:
                slab, passes = t // 2 + 1, (0, 1, 2) if t == 0 else (1, 2)
            if slab < SLABS:
                for c in passes:
                    turn_patches(slab, c)
                    if c != 1:
                        quantize_patches(slab, c // 2)
            if t == 0:
                for c in range(PASSES):
                    interleave(c, 1, nc.scalar.copy, 2)
                    quantize_comps(c, 1)
            for g, j in TURNED_AT.get(t, ()):
                turn_values(g, j)
                if j % 2 == 1:
                    quantize_values(g, j // 2)
            if t >= WEIGHT_LAG:
                times_weight(*slab_and_half(t - WEIGHT_LAG))

        for t in range(STEPS - WEIGHT_LAG, STEPS):
            times_weight(*slab_and_half(t))

        def turn_half(g, h):
            turn_values(g, 2 * h)
            turn_values(g, 2 * h + 1)
            quantize_values(g, h)

        turn_half(2, 0)
        for k in range(EARLY):
            contrast(1, k // FILTER_TILES, k % FILTER_TILES)
        turn_half(2, 1)
        for f in range(2):
            contrast(2, 0, f)
        turn_half(3, 0)
        for k in range(2, EARLY):
            contrast(2, k // FILTER_TILES, k % FILTER_TILES)
        turn_half(3, 1)
        for f in range(FILTER_TILES):
            contrast(3, 0, f)
            store(0, f)
        for f in range(EARLY - FILTER_TILES, FILTER_TILES):
            for g in range(GROUPS - 1):
                contrast(g, 1, f)
        for f in range(FILTER_TILES):
            contrast(3, 1, f)
            store(1, f)
